import numpy as np
import ml_dtypes


def mxq(x, axis, fmt="e4m3"):
    dtype, down = {"e4m3": (ml_dtypes.float8_e4m3fn, 7), "e5m2": (ml_dtypes.float8_e5m2, 14)}[fmt]
    v = np.moveaxis(np.asarray(x, np.float32).astype(ml_dtypes.bfloat16).astype(np.float64), axis, -1)
    blocks = v.reshape(v.shape[:-1] + (-1, 32))
    amax = np.abs(blocks).max(-1, keepdims=True)
    byte = np.maximum(np.where(amax > 0, np.frexp(amax)[1] - 1 + 127, 0) - down, 1)
    scale = np.exp2(byte - 127.0)
    codes = (blocks / scale).astype(np.float32).astype(dtype).astype(np.float64)
    return np.moveaxis((codes * scale).reshape(v.shape), -1, axis)


WIDE = False


def mx_kscale(k):
    if not WIDE:
        return np.ones(k)
    levels = np.array([10, -10, 5, -5, 0])
    if k % 512:
        return np.exp2(np.random.permutation(np.resize(levels, k // 32))).repeat(32)
    a = np.empty((k // 512, 16))
    for p in range(k // 512):
        a[p, :8] = np.random.permutation(np.resize(levels, 8))
        for g in range(8):
            far = levels[np.abs(levels - a[p, g]) >= 10]
            a[p, g + 8] = far[np.random.randint(len(far))]
    return np.exp2(a.ravel()).repeat(32)


def f64(x):
    return np.asarray(x).astype(np.float64)


def striped(idx):
    return np.tile(idx.reshape(-1, 16).T, (8, 1)).astype(np.uint16)


def unstriped(offs):
    return offs[:16].T.reshape(-1).astype(np.int64)


def pack_weight(w):
    k, n = w.shape
    w = f64(np.asarray(w, np.float32).astype(ml_dtypes.bfloat16)).reshape(k // 32, 32, n)
    amax = np.abs(w).max(1)
    byte = np.clip(np.where(amax > 0, np.frexp(amax)[1] - 1 + 127 - 7, 1), 1, 254)
    scaled = (w * np.exp2(127.0 - byte)[:, None, :]).reshape(k, n).astype(np.float32)
    words = np.ascontiguousarray(scaled.reshape(k // 512, 128, 4, n).transpose(0, 1, 3, 2)).astype(ml_dtypes.float8_e4m3fn).view(np.uint8)
    return words, np.ascontiguousarray(byte.astype(np.uint8).reshape(k // 512, 16, n))


def unpack_weight(words, scales):
    g, p, n, _ = words.shape
    vals = np.ascontiguousarray(words).view(ml_dtypes.float8_e4m3fn).astype(np.float64) * np.repeat(np.exp2(scales.astype(np.float64) - 127.0), 8, axis=1)[..., None]
    return vals.transpose(0, 1, 3, 2).reshape(g * 512, n)


def relu(v):
    return np.maximum(v, 0.0)


K, T, S, D, V, N = 512, 1024, 512, 2, 256, 128
P = 2 ** 7


def setup_inputs():
    n = np.random.standard_normal
    s = mx_kscale(K)[:, None]
    packed_w1 = pack_weight(n((K, N)) / np.sqrt(K) / s)
    return {
        "xT": (n((K, T)) * s).astype(np.float32),
        "w1_words": packed_w1[0],
        "w1_scales": packed_w1[1],
        "score": np.tile(np.random.standard_normal((D, 1, V)), (1, P, 1)).astype(np.float32),
        "offs": striped(np.random.permutation(T)[:S]),
        "pos1": striped(np.random.permutation(S)[:V]),
        "pos2": striped(np.random.permutation(S)[:V]),
    }


def reference(xT, w1_words, w1_scales, score, offs, pos1, pos2):
    xq = mxq(f64(xT)[:, unstriped(offs)], 0, "e4m3")
    y = unpack_weight(w1_words, w1_scales).T @ xq
    e0 = np.exp(f64(score)[0, :1])
    e1 = np.exp(f64(score)[1, :1])
    num = y[:, unstriped(pos1)] * e0 + y[:, unstriped(pos2)] * e1
    den = e0 + e1
    return relu(num / den)

@@ -1,0 +1,143 @@
+from contextlib import ExitStack
+
+import concourse.mybir as mybir
+from concourse.masks import make_identity
+
+K, T, S, V, M = 512, 1024, 512, 256, 128
+FLOPS = 2 * K * S * M + 4 * M * V
+
+F32 = mybir.dt.float32
+BF16 = mybir.dt.bfloat16
+I32 = mybir.dt.int32
+U32 = mybir.dt.uint32
+U16 = mybir.dt.uint16
+U8 = mybir.dt.uint8
+FP8X4 = mybir.dt.float8_e4m3fn_x4
+ACT = mybir.ActivationFunctionType
+ALU = mybir.AluOpType
+
+P = 128
+PACK = 4
+PIECE = 128
+PIECES = S // PIECE
+PER_COL = 16
+
+
+def tile_picked_gatv_relu_e_kernel(
+    tc, xT, w1_words, w1_scales, score, offs, pos1, pos2, out
+):
+    nc = tc.nc
+    with ExitStack() as ctx:
+        keep = ctx.enter_context(tc.tile_pool(name="keep", bufs=1))
+        psum = ctx.enter_context(tc.psum_pool(name="psum", bufs=1))
+
+        offs_sb = keep.tile([P, S // PER_COL], U16, name="offs_sb")
+        pos_sb = [keep.tile([P, V // PER_COL], U16, name=f"pos_sb{d}") for d in range(2)]
+        planes = [keep.tile([P, T], F32, name=f"plane{t}") for t in range(PACK)]
+        x_rows = xT.rearrange("(p t) n -> p t n", t=PACK)
+
+        nc.sync.dma_start(planes[0][:], x_rows[:, 0, :])
+        nc.sync.dma_start(offs_sb[:], offs)
+        for t in range(1, PACK):
+            nc.sync.dma_start(planes[t][:], x_rows[:, t, :])
+
+        sc = keep.tile([P, 2, 8], F32, name="sc")
+        nc.scalar.dma_start(sc[:, :, 0:2], score[:, 0, :].rearrange("d (p e) -> p d e", e=2))
+
+        w_words = keep.tile([P, M], U32, name="w_words", align_bytes=64)
+        w_scales = keep.tile([P, M], U8, name="w_scales", align_bytes=64)
+        nc.gpsimd.memset(w_scales[:].bitcast(I32), 0)
+        nc.sync.dma_start(w_words[:].bitcast(I32), w1_words[0].rearrange("p n t -> p (n t)").bitcast(I32))
+        for q in range(4):
+            nc.sync.dma_start(
+                w_scales[32 * q : 32 * q + 4, :].bitcast(I32), w1_scales[0, 4 * q : 4 * q + 4, :].bitcast(I32)
+            )
+        nc.sync.dma_start(pos_sb[0][:], pos1)
+        nc.sync.dma_start(pos_sb[1][:], pos2)
+
+        ident = keep.tile([P, P], F32, name="ident")
+        make_identity(nc, ident[:])
+
+        warm = keep.tile([P, 8], F32, name="warm")
+        nc.vector.memset(warm[:, 0:1], 0.0)
+        nc.scalar.activation(warm[:, 1:2], warm[:, 0:1], ACT.Sigmoid)
+
+        a_col = keep.tile([P, 2, 2], F32, name="a_col")
+        a_full = [keep.tile([P, V], F32, name=f"a_full{d}") for d in range(2)]
+        for d in range(2):
+            for e in range(2):
+                nc.scalar.activation(
+                    a_col[:, d, e : e + 1], sc[:, 1 - d, e : e + 1], ACT.Sigmoid, bias=sc[:, d, e : e + 1], scale=-1.0
+                )
+        for d in range(2):
+            spread = psum.tile([P, 2, P], F32, name=f"spread{d}")
+            for e in range(2):
+                nc.tensor.transpose(spread[:, e, :], a_col[:, d, e : e + 1].to_broadcast([P, P]), ident[:])
+            nc.scalar.copy(a_full[d][:].rearrange("m (p e) -> m p e", e=2), spread[:].rearrange("m e p -> m p e"))
+
+        picked = [keep.tile([P, 2, S], BF16, name=f"picked{u}") for u in range(2)]
+        woven = [keep.tile([P, PIECE, PACK], BF16, name=f"woven{c}", align_bytes=64) for c in range(PIECES)]
+        codes = [keep.tile([P, PIECE], U32, name=f"codes{c}", align_bytes=64) for c in range(PIECES)]
+        scales = [keep.tile([P, PIECE], U8, name=f"scales{c}", align_bytes=64) for c in range(PIECES)]
+        y = keep.tile([P, S], F32, name="y")
+
+        def gather(t, lo, hi):
+            nc.vector.tensor_copy(
+                picked[t // 2][:, t % 2, lo:hi], planes[t][:].indirect(offs_sb[:, lo // PER_COL : hi // PER_COL])
+            )
+
+        def weave(u, c, copy):
+            cols = slice(c * PIECE, (c + 1) * PIECE)
+            copy(woven[c][:, :, 2 * u : 2 * u + 2], picked[u][:, :, cols].rearrange("p e n -> p n e"))
+
+        def quantise(c):
+            nc.vector.quantize_mx(
+                out=codes[c][:].bitcast(FP8X4), scales=scales[c][:], in_=woven[c][:].rearrange("p n t -> p (n t)")
+            )
+
+        def project(c, copy):
+            acc = psum.tile([M, PIECE], F32, name=f"acc{c}")
+            nc.tensor.matmul_mx(
+                out=acc[:], lhsT=w_words[:].bitcast(FP8X4), lhsT_scale=w_scales[:],
+                rhs=codes[c][:].bitcast(FP8X4), rhs_scale=scales[c][:], start=True, stop=True,
+            )
+            copy(y[:, c * PIECE : (c + 1) * PIECE], acc[:])
+
+        gather(0, 0, S)
+        gather(1, 0, S // 2)
+        gather(1, S // 2, S)
+        for c in range(PIECES):
+            weave(0, c, nc.scalar.copy)
+        gather(2, 0, S)
+        for c in range(PIECES):
+            gather(3, c * PIECE, (c + 1) * PIECE)
+        for c in range(PIECES - 1):
+            weave(1, c, nc.scalar.copy)
+        quantise(0)
+        weave(1, 3, nc.vector.tensor_copy)
+        quantise(1)
+        quantise(3)
+        quantise(2)
+        project(0, nc.scalar.copy)
+        project(1, nc.scalar.copy)
+        project(3, nc.scalar.copy)
+        project(2, nc.vector.tensor_copy)
+
+        half = V // 2
+        terms = [[keep.tile([P, half], F32, name=f"term{h}_{d}") for d in range(2)] for h in range(2)]
+        total = [keep.tile([P, half], F32, name=f"total{h}") for h in range(2)]
+        result = [keep.tile([P, half], F32, name=f"result{h}") for h in range(2)]
+        for h in range(2):
+            for d in range(2):
+                nc.vector.tensor_tensor(
+                    terms[h][d][:],
+                    y[:].indirect(pos_sb[d][:, h * half // PER_COL : (h + 1) * half // PER_COL]),
+                    a_full[d][:, h * half : (h + 1) * half],
+                    ALU.mult,
+                )
+        for h in range(2):
+            nc.vector.tensor_tensor(total[h][:], terms[h][0][:], terms[h][1][:], ALU.add)
+        for h in range(2):
+            nc.vector.tensor_scalar_max(result[h][:], total[h][:], 0.0)
+        nc.sync.dma_start(out[:, 0:half], result[0][:])
+        nc.scalar.dma_start(out[:, half:V], result[1][:])

@@ -75,20 +75,25 @@ def tile_picked_gatv_relu_e_kernel(
                 nc.tensor.transpose(spread[:, e, :], a_col[:, d, e : e + 1].to_broadcast([P, P]), ident[:])
             nc.scalar.copy(a_full[d][:].rearrange("m (p e) -> m p e", e=2), spread[:].rearrange("m e p -> m p e"))
 
-        picked = [keep.tile([P, 2, S], BF16, name=f"picked{u}") for u in range(2)]
-        woven = [keep.tile([P, PIECE, PACK], BF16, name=f"woven{c}", align_bytes=64) for c in range(PIECES)]
-        codes = [keep.tile([P, PIECE], U32, name=f"codes{c}", align_bytes=64) for c in range(PIECES)]
-        scales = [keep.tile([P, PIECE], U8, name=f"scales{c}", align_bytes=64) for c in range(PIECES)]
+        bounds = [0, 64, 192, 320, 448, 512]
+        pieces = [slice(lo, hi) for lo, hi in zip(bounds, bounds[1:])]
+        widths = [hi - lo for lo, hi in zip(bounds, bounds[1:])]
+        on_vector = 2
+        on_scalar = [c for c in range(len(pieces)) if c != on_vector]
+        picked = keep.tile([P, PACK, S], BF16, name="picked")
+        woven = [keep.tile([P, n, PACK], BF16, name=f"woven{c}", align_bytes=64) for c, n in enumerate(widths)]
+        codes = [keep.tile([P, n], U32, name=f"codes{c}", align_bytes=64) for c, n in enumerate(widths)]
+        scales = [keep.tile([P, n], U8, name=f"scales{c}", align_bytes=64) for c, n in enumerate(widths)]
         y = keep.tile([P, S], F32, name="y")
 
-        def gather(t, lo, hi):
-            nc.vector.tensor_copy(
-                picked[t // 2][:, t % 2, lo:hi], planes[t][:].indirect(offs_sb[:, lo // PER_COL : hi // PER_COL])
-            )
+        def looked_up(t, lo, hi):
+            return planes[t][:].indirect(offs_sb[:, lo // PER_COL : hi // PER_COL])
 
-        def weave(u, c, copy):
-            cols = slice(c * PIECE, (c + 1) * PIECE)
-            copy(woven[c][:, :, 2 * u : 2 * u + 2], picked[u][:, :, cols].rearrange("p e n -> p n e"))
+        def gather(t, lo, hi):
+            nc.vector.tensor_copy(picked[:, t, lo:hi], looked_up(t, lo, hi))
+
+        def weave(u, c):
+            nc.scalar.copy(woven[c][:, :, 2 * u : 2 * u + 2], picked[:, 2 * u : 2 * u + 2, pieces[c]].rearrange("p e n -> p n e"))
 
         def quantise(c):
             nc.vector.quantize_mx(
@@ -96,48 +101,45 @@ def tile_picked_gatv_relu_e_kernel(
             )
 
         def project(c, copy):
-            acc = psum.tile([M, PIECE], F32, name=f"acc{c}")
+            acc = psum.tile([M, widths[c]], F32, name=f"acc{c}")
             nc.tensor.matmul_mx(
                 out=acc[:], lhsT=w_words[:].bitcast(FP8X4), lhsT_scale=w_scales[:],
                 rhs=codes[c][:].bitcast(FP8X4), rhs_scale=scales[c][:], start=True, stop=True,
             )
-            copy(y[:, c * PIECE : (c + 1) * PIECE], acc[:])
+            copy(y[:, pieces[c]], acc[:])
 
         gather(0, 0, S)
-        gather(1, 0, S // 2)
-        gather(1, S // 2, S)
-        for c in range(PIECES):
-            weave(0, c, nc.scalar.copy)
+        gather(1, 0, bounds[2])
+        gather(1, bounds[2], S)
+        for c in on_scalar:
+            weave(0, c)
         gather(2, 0, S)
-        for c in range(PIECES):
-            gather(3, c * PIECE, (c + 1) * PIECE)
-        for c in range(PIECES - 1):
-            weave(1, c, nc.scalar.copy)
-        quantise(0)
-        weave(1, 3, nc.vector.tensor_copy)
-        quantise(1)
-        quantise(3)
-        quantise(2)
-        project(0, nc.scalar.copy)
-        project(1, nc.scalar.copy)
-        project(3, nc.scalar.copy)
-        project(2, nc.vector.tensor_copy)
+        for c in range(len(pieces)):
+            gather(3, bounds[c], bounds[c + 1])
+        for c in on_scalar:
+            weave(1, c)
+        nc.vector.tensor_copy(woven[on_vector][:], picked[:, :, pieces[on_vector]].rearrange("p t n -> p n t"))
+        for c in range(len(pieces)):
+            quantise(c)
+        for c in range(len(pieces)):
+            project(c, nc.vector.tensor_copy if c == len(pieces) - 1 else nc.scalar.copy)
 
-        half = V // 2
-        terms = [[keep.tile([P, half], F32, name=f"term{h}_{d}") for d in range(2)] for h in range(2)]
-        total = [keep.tile([P, half], F32, name=f"total{h}") for h in range(2)]
-        result = [keep.tile([P, half], F32, name=f"result{h}") for h in range(2)]
-        for h in range(2):
+        cuts = [0, 192, V]
+        parts = list(zip(cuts, cuts[1:]))
+        terms = [[keep.tile([P, hi - lo], F32, name=f"term{lo}_{d}") for d in range(2)] for lo, hi in parts]
+        total = [keep.tile([P, hi - lo], F32, name=f"total{lo}") for lo, hi in parts]
+        result = [keep.tile([P, hi - lo], F32, name=f"result{lo}") for lo, hi in parts]
+        for h, (lo, hi) in enumerate(parts):
             for d in range(2):
                 nc.vector.tensor_tensor(
                     terms[h][d][:],
-                    y[:].indirect(pos_sb[d][:, h * half // PER_COL : (h + 1) * half // PER_COL]),
-                    a_full[d][:, h * half : (h + 1) * half],
+                    y[:].indirect(pos_sb[d][:, lo // PER_COL : hi // PER_COL]),
+                    a_full[d][:, lo:hi],
                     ALU.mult,
                 )
         for h in range(2):
             nc.vector.tensor_tensor(total[h][:], terms[h][0][:], terms[h][1][:], ALU.add)
         for h in range(2):
             nc.vector.tensor_scalar_max(result[h][:], total[h][:], 0.0)
-        nc.sync.dma_start(out[:, 0:half], result[0][:])
-        nc.scalar.dma_start(out[:, half:V], result[1][:])
+        nc.sync.dma_start(out[:, cuts[0] : cuts[1]], result[0][:])
+        nc.scalar.dma_start(out[:, cuts[1] : cuts[2]], result[1][:])

@@ -75,12 +75,12 @@ def tile_picked_gatv_relu_e_kernel(
                 nc.tensor.transpose(spread[:, e, :], a_col[:, d, e : e + 1].to_broadcast([P, P]), ident[:])
             nc.scalar.copy(a_full[d][:].rearrange("m (p e) -> m p e", e=2), spread[:].rearrange("m e p -> m p e"))
 
-        bounds = [0, 64, 192, 320, 448, 512]
+        bounds = [0, 128, 256, 384, 448, 512]
         pieces = [slice(lo, hi) for lo, hi in zip(bounds, bounds[1:])]
         widths = [hi - lo for lo, hi in zip(bounds, bounds[1:])]
         on_vector = 2
         on_scalar = [c for c in range(len(pieces)) if c != on_vector]
-        picked = keep.tile([P, PACK, S], BF16, name="picked")
+        picked = keep.tile([P, PACK, S], F32, name="picked")
         woven = [keep.tile([P, n, PACK], BF16, name=f"woven{c}", align_bytes=64) for c, n in enumerate(widths)]
         codes = [keep.tile([P, n], U32, name=f"codes{c}", align_bytes=64) for c, n in enumerate(widths)]
         scales = [keep.tile([P, n], U8, name=f"scales{c}", align_bytes=64) for c, n in enumerate(widths)]
@@ -114,8 +114,8 @@ def tile_picked_gatv_relu_e_kernel(
         for c in on_scalar:
             weave(0, c)
         gather(2, 0, S)
-        for c in range(len(pieces)):
-            gather(3, bounds[c], bounds[c + 1])
+        for lo in range(0, S, 128):
+            gather(3, lo, lo + 128)
         for c in on_scalar:
             weave(1, c)
         nc.vector.tensor_copy(woven[on_vector][:], picked[:, :, pieces[on_vector]].rearrange("p t n -> p n t"))

@@ -38,11 +38,12 @@ def tile_picked_gatv_relu_e_kernel(
 
         nc.sync.dma_start(planes[0][:], x_rows[:, 0, :])
         nc.sync.dma_start(offs_sb[:], offs)
-        for t in range(1, PACK):
+        nc.sync.dma_start(planes[1][:], x_rows[:, 1, :])
+        sc = keep.tile([P, 2, 8], F32, name="sc")
+        nc.sync.dma_start(sc[:, :, 0:2], score[:, 0, :].rearrange("d (p e) -> p d e", e=2))
+        for t in range(2, PACK):
             nc.sync.dma_start(planes[t][:], x_rows[:, t, :])
 
-        sc = keep.tile([P, 2, 8], F32, name="sc")
-        nc.scalar.dma_start(sc[:, :, 0:2], score[:, 0, :].rearrange("d (p e) -> p d e", e=2))
 
         w_words = keep.tile([P, M], U32, name="w_words", align_bytes=64)
         w_scales = keep.tile([P, M], U8, name="w_scales", align_bytes=64)
@@ -62,25 +63,13 @@ def tile_picked_gatv_relu_e_kernel(
         nc.vector.memset(warm[:, 0:1], 0.0)
         nc.scalar.activation(warm[:, 1:2], warm[:, 0:1], ACT.Sigmoid)
 
-        a_col = keep.tile([P, 2, 2], F32, name="a_col")
-        a_full = [keep.tile([P, V], F32, name=f"a_full{d}") for d in range(2)]
-        for d in range(2):
-            for e in range(2):
-                nc.scalar.activation(
-                    a_col[:, d, e : e + 1], sc[:, 1 - d, e : e + 1], ACT.Sigmoid, bias=sc[:, d, e : e + 1], scale=-1.0
-                )
-        for d in range(2):
-            spread = psum.tile([P, 2, P], F32, name=f"spread{d}")
-            for e in range(2):
-                nc.tensor.transpose(spread[:, e, :], a_col[:, d, e : e + 1].to_broadcast([P, P]), ident[:])
-            nc.scalar.copy(a_full[d][:].rearrange("m (p e) -> m p e", e=2), spread[:].rearrange("m e p -> m p e"))
-
         bounds = [0, 128, 256, 384, 448, 512]
         pieces = [slice(lo, hi) for lo, hi in zip(bounds, bounds[1:])]
         widths = [hi - lo for lo, hi in zip(bounds, bounds[1:])]
         on_vector = 2
         on_scalar = [c for c in range(len(pieces)) if c != on_vector]
-        picked = keep.tile([P, PACK, S], F32, name="picked")
+        picked = keep.tile([P, PACK, S], BF16, name="picked", tag="picked")
+        rounded = keep.tile([P, T], BF16, name="rounded")
         woven = [keep.tile([P, n, PACK], BF16, name=f"woven{c}", align_bytes=64) for c, n in enumerate(widths)]
         codes = [keep.tile([P, n], U32, name=f"codes{c}", align_bytes=64) for c, n in enumerate(widths)]
         scales = [keep.tile([P, n], U8, name=f"scales{c}", align_bytes=64) for c, n in enumerate(widths)]
@@ -108,7 +97,19 @@ def tile_picked_gatv_relu_e_kernel(
             )
             copy(y[:, pieces[c]], acc[:])
 
-        gather(0, 0, S)
+        nc.scalar.copy(rounded[:], planes[0][:])
+        gather(0, 0, 384)
+        nc.scalar.activation(picked[:, 0, 384:S], rounded[:].indirect(offs_sb[:, 384 // PER_COL :]), ACT.Copy)
+        a_col = keep.tile([P, 2, 2], F32, name="a_col")
+        for d in range(2):
+            for e in range(2):
+                nc.scalar.activation(
+                    a_col[:, d, e : e + 1], sc[:, 1 - d, e : e + 1], ACT.Sigmoid, bias=sc[:, d, e : e + 1], scale=-1.0
+                )
+        spread = [psum.tile([P, 2, P], F32, name=f"spread{d}") for d in range(2)]
+        for d in range(2):
+            for e in range(2):
+                nc.tensor.transpose(spread[d][:, e, :], a_col[:, d, e : e + 1].to_broadcast([P, P]), ident[:])
         gather(1, 0, bounds[2])
         gather(1, bounds[2], S)
         for c in on_scalar:
@@ -121,24 +122,30 @@ def tile_picked_gatv_relu_e_kernel(
         nc.vector.tensor_copy(woven[on_vector][:], picked[:, :, pieces[on_vector]].rearrange("p t n -> p n t"))
         for c in range(len(pieces)):
             quantise(c)
+        a_both = keep.tile([P, 2, V], F32, name="a_both", tag="picked")
+        a_full = [a_both[:, d, :] for d in range(2)]
+
+        def spread_out(d, copy):
+            copy(a_full[d].rearrange("m (p e) -> m p e", e=2), spread[d][:].rearrange("m e p -> m p e"))
+
+        spread_out(0, nc.vector.tensor_copy)
         for c in range(len(pieces)):
             project(c, nc.vector.tensor_copy if c == len(pieces) - 1 else nc.scalar.copy)
+        spread_out(1, nc.scalar.copy)
 
         cuts = [0, 192, V]
         parts = list(zip(cuts, cuts[1:]))
-        terms = [[keep.tile([P, hi - lo], F32, name=f"term{lo}_{d}") for d in range(2)] for lo, hi in parts]
+        first = keep.tile([P, V], F32, name="first")
+        second = [keep.tile([P, hi - lo], F32, name=f"second{lo}") for lo, hi in parts]
         total = [keep.tile([P, hi - lo], F32, name=f"total{lo}") for lo, hi in parts]
         result = [keep.tile([P, hi - lo], F32, name=f"result{lo}") for lo, hi in parts]
+        nc.vector.tensor_tensor(first[:], y[:].indirect(pos_sb[0][:]), a_full[0], ALU.mult)
         for h, (lo, hi) in enumerate(parts):
-            for d in range(2):
-                nc.vector.tensor_tensor(
-                    terms[h][d][:],
-                    y[:].indirect(pos_sb[d][:, lo // PER_COL : hi // PER_COL]),
-                    a_full[d][:, lo:hi],
-                    ALU.mult,
-                )
-        for h in range(2):
-            nc.vector.tensor_tensor(total[h][:], terms[h][0][:], terms[h][1][:], ALU.add)
+            nc.vector.tensor_tensor(
+                second[h][:], y[:].indirect(pos_sb[1][:, lo // PER_COL : hi // PER_COL]), a_full[1][:, lo:hi], ALU.mult
+            )
+        for h, (lo, hi) in enumerate(parts):
+            nc.vector.tensor_tensor(total[h][:], first[:, lo:hi], second[h][:], ALU.add)
         for h in range(2):
             nc.vector.tensor_scalar_max(result[h][:], total[h][:], 0.0)
         nc.sync.dma_start(out[:, cuts[0] : cuts[1]], result[0][:])

@@ -66,27 +66,30 @@ def tile_picked_gatv_relu_e_kernel(
         bounds = [0, 128, 256, 384, 448, 512]
         pieces = [slice(lo, hi) for lo, hi in zip(bounds, bounds[1:])]
         widths = [hi - lo for lo, hi in zip(bounds, bounds[1:])]
-        on_vector = 2
-        on_scalar = [c for c in range(len(pieces)) if c != on_vector]
-        picked = keep.tile([P, PACK, S], BF16, name="picked", tag="picked")
-        rounded = keep.tile([P, T], BF16, name="rounded")
-        woven = [keep.tile([P, n, PACK], BF16, name=f"woven{c}", align_bytes=64) for c, n in enumerate(widths)]
-        codes = [keep.tile([P, n], U32, name=f"codes{c}", align_bytes=64) for c, n in enumerate(widths)]
+        picked = keep.tile([P, 2, S, 2], BF16, name="picked")
+        rounded = [keep.tile([P, T], BF16, name=f"rounded{t}") for t in range(2)]
+        woven = [keep.tile([P, n, 2], U32, name=f"woven{c}", tag=f"woven{c}", align_bytes=64) for c, n in enumerate(widths)]
+        codes = [keep.tile([P, n], U32, name=f"codes{c}", tag=f"codes{c}", align_bytes=64) for c, n in enumerate(widths)]
         scales = [keep.tile([P, n], U8, name=f"scales{c}", align_bytes=64) for c, n in enumerate(widths)]
         y = keep.tile([P, S], F32, name="y")
 
-        def looked_up(t, lo, hi):
-            return planes[t][:].indirect(offs_sb[:, lo // PER_COL : hi // PER_COL])
+        def entries(lo, hi):
+            return offs_sb[:, lo // PER_COL : hi // PER_COL]
 
         def gather(t, lo, hi):
-            nc.vector.tensor_copy(picked[:, t, lo:hi], looked_up(t, lo, hi))
+            nc.vector.tensor_copy(picked[:, t // 2, lo:hi, t % 2], planes[t][:].indirect(entries(lo, hi)))
 
-        def weave(u, c):
-            nc.scalar.copy(woven[c][:, :, 2 * u : 2 * u + 2], picked[:, 2 * u : 2 * u + 2, pieces[c]].rearrange("p e n -> p n e"))
+        def gather_rounded(t, lo, hi):
+            nc.scalar.copy(rounded[t][:], planes[t][:])
+            nc.scalar.activation(picked[:, t // 2, lo:hi, t % 2], rounded[t][:].indirect(entries(lo, hi)), ACT.Copy)
+
+        def weave(c):
+            words = picked[:].rearrange("p u n e -> p u (n e)").bitcast(U32)
+            nc.scalar.copy(woven[c][:], words[:, :, pieces[c]].rearrange("p u n -> p n u"))
 
         def quantise(c):
             nc.vector.quantize_mx(
-                out=codes[c][:].bitcast(FP8X4), scales=scales[c][:], in_=woven[c][:].rearrange("p n t -> p (n t)")
+                out=codes[c][:].bitcast(FP8X4), scales=scales[c][:], in_=woven[c][:].rearrange("p n u -> p (n u)").bitcast(BF16)
             )
 
         def project(c, copy):
@@ -97,9 +100,9 @@ def tile_picked_gatv_relu_e_kernel(
             )
             copy(y[:, pieces[c]], acc[:])
 
-        nc.scalar.copy(rounded[:], planes[0][:])
-        gather(0, 0, 384)
-        nc.scalar.activation(picked[:, 0, 384:S], rounded[:].indirect(offs_sb[:, 384 // PER_COL :]), ACT.Copy)
+        share = 384
+        gather(0, 0, share)
+        gather_rounded(0, share, S)
         a_col = keep.tile([P, 2, 2], F32, name="a_col")
         for d in range(2):
             for e in range(2):
@@ -110,23 +113,20 @@ def tile_picked_gatv_relu_e_kernel(
         for d in range(2):
             for e in range(2):
                 nc.tensor.transpose(spread[d][:, e, :], a_col[:, d, e : e + 1].to_broadcast([P, P]), ident[:])
-        gather(1, 0, bounds[2])
-        gather(1, bounds[2], S)
-        for c in on_scalar:
-            weave(0, c)
+        gather(1, 0, share)
+        gather_rounded(1, share, S)
         gather(2, 0, S)
         for lo in range(0, S, 128):
             gather(3, lo, lo + 128)
-        for c in on_scalar:
-            weave(1, c)
-        nc.vector.tensor_copy(woven[on_vector][:], picked[:, :, pieces[on_vector]].rearrange("p t n -> p n t"))
+        for c in range(len(pieces)):
+            weave(c)
         for c in range(len(pieces)):
             quantise(c)
-        a_both = keep.tile([P, 2, V], F32, name="a_both", tag="picked")
-        a_full = [a_both[:, d, :] for d in range(2)]
+        held_by = [f"woven{len(pieces) - 1}", f"codes{len(pieces) - 2}"]
+        a_full = [keep.tile([P, V], F32, name=f"a_full{d}", tag=held_by[d], align_bytes=64) for d in range(2)]
 
         def spread_out(d, copy):
-            copy(a_full[d].rearrange("m (p e) -> m p e", e=2), spread[d][:].rearrange("m e p -> m p e"))
+            copy(a_full[d][:].rearrange("m (p e) -> m p e", e=2), spread[d][:].rearrange("m e p -> m p e"))
 
         spread_out(0, nc.vector.tensor_copy)
         for c in range(len(pieces)):
@@ -139,7 +139,7 @@ def tile_picked_gatv_relu_e_kernel(
         second = [keep.tile([P, hi - lo], F32, name=f"second{lo}") for lo, hi in parts]
         total = [keep.tile([P, hi - lo], F32, name=f"total{lo}") for lo, hi in parts]
         result = [keep.tile([P, hi - lo], F32, name=f"result{lo}") for lo, hi in parts]
-        nc.vector.tensor_tensor(first[:], y[:].indirect(pos_sb[0][:]), a_full[0], ALU.mult)
+        nc.vector.tensor_tensor(first[:], y[:].indirect(pos_sb[0][:]), a_full[0][:], ALU.mult)
         for h, (lo, hi) in enumerate(parts):
             nc.vector.tensor_tensor(
                 second[h][:], y[:].indirect(pos_sb[1][:, lo // PER_COL : hi // PER_COL]), a_full[1][:, lo:hi], ALU.mult

@@ -36,12 +36,12 @@ def tile_picked_gatv_relu_e_kernel(
         planes = [keep.tile([P, T], F32, name=f"plane{t}") for t in range(PACK)]
         x_rows = xT.rearrange("(p t) n -> p t n", t=PACK)
 
-        nc.sync.dma_start(planes[0][:], x_rows[:, 0, :])
+        nc.sync.dma_start(planes[2][:], x_rows[:, 2, :])
         nc.sync.dma_start(offs_sb[:], offs)
-        nc.sync.dma_start(planes[1][:], x_rows[:, 1, :])
         sc = keep.tile([P, 2, 8], F32, name="sc")
         nc.sync.dma_start(sc[:, :, 0:2], score[:, 0, :].rearrange("d (p e) -> p d e", e=2))
-        for t in range(2, PACK):
+        nc.sync.dma_start(planes[0][:], x_rows[:, 0, :])
+        for t in (1, 3):
             nc.sync.dma_start(planes[t][:], x_rows[:, t, :])
 
 
@@ -101,8 +101,6 @@ def tile_picked_gatv_relu_e_kernel(
             copy(y[:, pieces[c]], acc[:])
 
         share = 384
-        gather(0, 0, share)
-        gather_rounded(0, share, S)
         a_col = keep.tile([P, 2, 2], F32, name="a_col")
         for d in range(2):
             for e in range(2):
@@ -113,9 +111,11 @@ def tile_picked_gatv_relu_e_kernel(
         for d in range(2):
             for e in range(2):
                 nc.tensor.transpose(spread[d][:, e, :], a_col[:, d, e : e + 1].to_broadcast([P, P]), ident[:])
+        gather(2, 0, S)
+        gather(0, 0, share)
+        gather_rounded(0, share, S)
         gather(1, 0, share)
         gather_rounded(1, share, S)
-        gather(2, 0, S)
         for lo in range(0, S, 128):
             gather(3, lo, lo + 128)
         for c in range(len(pieces)):

@@ -38,8 +38,8 @@ def tile_picked_gatv_relu_e_kernel(
 
         nc.sync.dma_start(planes[2][:], x_rows[:, 2, :])
         nc.sync.dma_start(offs_sb[:], offs)
-        sc = keep.tile([P, 2, 8], F32, name="sc")
-        nc.sync.dma_start(sc[:, :, 0:2], score[:, 0, :].rearrange("d (p e) -> p d e", e=2))
+        sc = keep.tile([P // 2, 2, 8], F32, name="sc")
+        nc.sync.dma_start(sc[:, :, 0:4], score[:, 0, :].rearrange("d (p e) -> p d e", e=4))
         nc.sync.dma_start(planes[0][:], x_rows[:, 0, :])
         for t in (1, 3):
             nc.sync.dma_start(planes[t][:], x_rows[:, t, :])
@@ -101,15 +101,16 @@ def tile_picked_gatv_relu_e_kernel(
             copy(y[:, pieces[c]], acc[:])
 
         share = 384
-        a_col = keep.tile([P, 2, 2], F32, name="a_col")
+        a_col = keep.tile([P, 2, 4], F32, name="a_col")
+        nc.vector.memset(a_col[P // 2 :], 0.0)
         for d in range(2):
-            for e in range(2):
+            for e in range(4):
                 nc.scalar.activation(
-                    a_col[:, d, e : e + 1], sc[:, 1 - d, e : e + 1], ACT.Sigmoid, bias=sc[:, d, e : e + 1], scale=-1.0
+                    a_col[: P // 2, d, e : e + 1], sc[:, 1 - d, e : e + 1], ACT.Sigmoid, bias=sc[:, d, e : e + 1], scale=-1.0
                 )
-        spread = [psum.tile([P, 2, P], F32, name=f"spread{d}") for d in range(2)]
+        spread = [psum.tile([P, 4, P], F32, name=f"spread{d}") for d in range(2)]
         for d in range(2):
-            for e in range(2):
+            for e in range(4):
                 nc.tensor.transpose(spread[d][:, e, :], a_col[:, d, e : e + 1].to_broadcast([P, P]), ident[:])
         gather(2, 0, S)
         gather(0, 0, share)
@@ -126,7 +127,7 @@ def tile_picked_gatv_relu_e_kernel(
         a_full = [keep.tile([P, V], F32, name=f"a_full{d}", tag=held_by[d], align_bytes=64) for d in range(2)]
 
         def spread_out(d, copy):
-            copy(a_full[d][:].rearrange("m (p e) -> m p e", e=2), spread[d][:].rearrange("m e p -> m p e"))
+            copy(a_full[d][:].rearrange("m (p e) -> m p e", e=4), spread[d][:, :, : P // 2].rearrange("m e p -> m p e"))
 
         spread_out(0, nc.vector.tensor_copy)
         for c in range(len(pieces)):

@@ -59,10 +59,6 @@ def tile_picked_gatv_relu_e_kernel(
         ident = keep.tile([P, P], F32, name="ident")
         make_identity(nc, ident[:])
 
-        warm = keep.tile([P, 8], F32, name="warm")
-        nc.vector.memset(warm[:, 0:1], 0.0)
-        nc.scalar.activation(warm[:, 1:2], warm[:, 0:1], ACT.Sigmoid)
-
         bounds = [0, 128, 256, 384, 448, 512]
         pieces = [slice(lo, hi) for lo, hi in zip(bounds, bounds[1:])]
         widths = [hi - lo for lo, hi in zip(bounds, bounds[1:])]

@@ -21,6 +21,7 @@ PACK = 4
 PIECE = 128
 PIECES = S // PIECE
 PER_COL = 16
+FLOOR = 2.0**-26
 
 
 def tile_picked_gatv_relu_e_kernel(
@@ -98,12 +99,14 @@ def tile_picked_gatv_relu_e_kernel(
 
         share = 384
         a_col = keep.tile([P, 2, 4], F32, name="a_col")
-        nc.vector.memset(a_col[P // 2 :], 0.0)
-        for d in range(2):
-            for e in range(4):
-                nc.scalar.activation(
-                    a_col[: P // 2, d, e : e + 1], sc[:, 1 - d, e : e + 1], ACT.Sigmoid, bias=sc[:, d, e : e + 1], scale=-1.0
-                )
+        nc.gpsimd.memset(a_col[P // 2 :], 0.0)
+        raw = keep.tile([P // 2, 4], F32, name="raw")
+        minus_one = keep.tile([P // 2, 4], F32, name="minus_one")
+        nc.gpsimd.memset(minus_one[:], -1.0)
+        for e in range(4):
+            nc.scalar.activation(raw[:, e : e + 1], sc[:, 0, e : e + 1], ACT.Sigmoid, bias=sc[:, 1, e : e + 1], scale=-1.0)
+        nc.gpsimd.tensor_scalar(a_col[: P // 2, 1, :], raw[:], FLOOR, 1.0, ALU.max, ALU.mult)
+        nc.gpsimd.tensor_tensor(a_col[: P // 2, 0, :], a_col[: P // 2, 1, :], minus_one[:], ALU.pow)
         spread = [psum.tile([P, 4, P], F32, name=f"spread{d}") for d in range(2)]
         for d in range(2):
             for e in range(4):
@@ -119,31 +122,31 @@ def tile_picked_gatv_relu_e_kernel(
             weave(c)
         for c in range(len(pieces)):
             quantise(c)
-        held_by = [f"woven{len(pieces) - 1}", f"codes{len(pieces) - 2}"]
-        a_full = [keep.tile([P, V], F32, name=f"a_full{d}", tag=held_by[d], align_bytes=64) for d in range(2)]
-
-        def spread_out(d, copy):
-            copy(a_full[d][:].rearrange("m (p e) -> m p e", e=4), spread[d][:, :, : P // 2].rearrange("m e p -> m p e"))
-
-        spread_out(0, nc.vector.tensor_copy)
+        ratio = keep.tile([P, V], F32, name="ratio", tag=f"woven{len(pieces) - 1}", align_bytes=64)
+        nc.vector.tensor_scalar_add(
+            ratio[:].rearrange("m (p e) -> m p e", e=4), spread[0][:, :, : P // 2].rearrange("m e p -> m p e"), -1.0
+        )
         for c in range(len(pieces)):
             project(c, nc.vector.tensor_copy if c == len(pieces) - 1 else nc.scalar.copy)
-        spread_out(1, nc.scalar.copy)
 
         cuts = [0, 192, V]
         parts = list(zip(cuts, cuts[1:]))
-        first = keep.tile([P, V], F32, name="first")
-        second = [keep.tile([P, hi - lo], F32, name=f"second{lo}") for lo, hi in parts]
+        first = [keep.tile([P, hi - lo], F32, name=f"first{lo}") for lo, hi in parts]
         total = [keep.tile([P, hi - lo], F32, name=f"total{lo}") for lo, hi in parts]
         result = [keep.tile([P, hi - lo], F32, name=f"result{lo}") for lo, hi in parts]
-        nc.vector.tensor_tensor(first[:], y[:].indirect(pos_sb[0][:]), a_full[0][:], ALU.mult)
         for h, (lo, hi) in enumerate(parts):
             nc.vector.tensor_tensor(
-                second[h][:], y[:].indirect(pos_sb[1][:, lo // PER_COL : hi // PER_COL]), a_full[1][:, lo:hi], ALU.mult
+                first[h][:], y[:].indirect(pos_sb[0][:, lo // PER_COL : hi // PER_COL]), ratio[:, lo:hi], ALU.mult
             )
         for h, (lo, hi) in enumerate(parts):
-            nc.vector.tensor_tensor(total[h][:], first[:, lo:hi], second[h][:], ALU.add)
-        for h in range(2):
-            nc.vector.tensor_scalar_max(result[h][:], total[h][:], 0.0)
+            nc.vector.tensor_tensor(
+                total[h][:], y[:].indirect(pos_sb[1][:, lo // PER_COL : hi // PER_COL]), first[h][:], ALU.add
+            )
+        weight = spread[1][:, :, : P // 2].rearrange("m e p -> m p e")
+        for h, (lo, hi) in enumerate(parts):
+            nc.vector.scalar_tensor_tensor(
+                result[h][:].rearrange("m (p e) -> m p e", e=4), total[h][:].rearrange("m (p e) -> m p e", e=4), 0.0,
+                weight[:, lo // 4 : hi // 4, :], ALU.max, ALU.mult,
+            )
         nc.sync.dma_start(out[:, cuts[0] : cuts[1]], result[0][:])
         nc.scalar.dma_start(out[:, cuts[1] : cuts[2]], result[1][:])

@@ -30,6 +30,7 @@ def tile_picked_gatv_relu_e_kernel(
     nc = tc.nc
     with ExitStack() as ctx:
         keep = ctx.enter_context(tc.tile_pool(name="keep", bufs=1))
+        reuse = ctx.enter_context(tc.tile_pool(name="reuse", bufs=1))
         psum = ctx.enter_context(tc.psum_pool(name="psum", bufs=1))
 
         offs_sb = keep.tile([P, S // PER_COL], U16, name="offs_sb")
@@ -63,10 +64,19 @@ def tile_picked_gatv_relu_e_kernel(
         bounds = [0, 128, 256, 384, 448, 512]
         pieces = [slice(lo, hi) for lo, hi in zip(bounds, bounds[1:])]
         widths = [hi - lo for lo, hi in zip(bounds, bounds[1:])]
-        picked = keep.tile([P, 2, S, 2], BF16, name="picked")
+        head = bounds[1]
+        picked = {
+            0: reuse.tile([P, 2, head, 2], BF16, name="picked_head", offset=0, align_bytes=64),
+            head: keep.tile([P, 2, S - head, 2], BF16, name="picked_rest"),
+        }
+
+        def pairs(lo, hi):
+            start = 0 if lo < head else head
+            return picked[start][:, :, lo - start : hi - start, :]
+
         rounded = [keep.tile([P, T], BF16, name=f"rounded{t}") for t in range(2)]
-        woven = [keep.tile([P, n, 2], U32, name=f"woven{c}", tag=f"woven{c}", align_bytes=64) for c, n in enumerate(widths)]
-        codes = [keep.tile([P, n], U32, name=f"codes{c}", tag=f"codes{c}", align_bytes=64) for c, n in enumerate(widths)]
+        woven = [keep.tile([P, n, 2], U32, name=f"woven{c}", tag=f"woven{c}", align_bytes=64) for c, n in enumerate(widths[:-1])]
+        codes = [keep.tile([P, n], U32, name=f"codes{c}", tag=f"codes{c}", align_bytes=64) for c, n in enumerate(widths[:-1])]
         scales = [keep.tile([P, n], U8, name=f"scales{c}", align_bytes=64) for c, n in enumerate(widths)]
         y = keep.tile([P, S], F32, name="y")
 
@@ -74,15 +84,15 @@ def tile_picked_gatv_relu_e_kernel(
             return offs_sb[:, lo // PER_COL : hi // PER_COL]
 
         def gather(t, lo, hi):
-            nc.vector.tensor_copy(picked[:, t // 2, lo:hi, t % 2], planes[t][:].indirect(entries(lo, hi)))
+            nc.vector.tensor_copy(pairs(lo, hi)[:, t // 2, :, t % 2], planes[t][:].indirect(entries(lo, hi)))
 
         def gather_rounded(t, lo, hi):
             nc.scalar.copy(rounded[t][:], planes[t][:])
-            nc.scalar.activation(picked[:, t // 2, lo:hi, t % 2], rounded[t][:].indirect(entries(lo, hi)), ACT.Copy)
+            nc.scalar.activation(pairs(lo, hi)[:, t // 2, :, t % 2], rounded[t][:].indirect(entries(lo, hi)), ACT.Copy)
 
-        def weave(c):
-            words = picked[:].rearrange("p u n e -> p u (n e)").bitcast(U32)
-            nc.scalar.copy(woven[c][:], words[:, :, pieces[c]].rearrange("p u n -> p n u"))
+        def weave(c, copy, word):
+            words = pairs(bounds[c], bounds[c + 1]).rearrange("p u n e -> p u (n e)").bitcast(word)
+            copy(woven[c][:].bitcast(word), words.rearrange("p u n -> p n u"))
 
         def quantise(c):
             nc.vector.quantize_mx(
@@ -111,25 +121,32 @@ def tile_picked_gatv_relu_e_kernel(
         for d in range(2):
             for e in range(4):
                 nc.tensor.transpose(spread[d][:, e, :], a_col[:, d, e : e + 1].to_broadcast([P, P]), ident[:])
-        gather(2, 0, S)
-        gather(0, 0, share)
-        gather_rounded(0, share, S)
-        gather(1, 0, share)
-        gather_rounded(1, share, S)
+        gather(2, 0, head)
+        gather(2, head, S)
+        for t in range(2):
+            gather(t, 0, head)
+            gather(t, head, share)
+            gather_rounded(t, share, S)
         for lo in range(0, S, 128):
             gather(3, lo, lo + 128)
-        for c in range(len(pieces)):
-            weave(c)
-        for c in range(len(pieces)):
+        for c in range(4):
+            weave(c, nc.scalar.copy, U32)
+        quantise(0)
+        woven.append(reuse.tile([P, widths[4], 2], U32, name="woven4", offset=0, align_bytes=64))
+        weave(4, nc.vector.tensor_copy, I32)
+        order = [0, 1, 2, 4, 3]
+        quantise(1)
+        codes.append(keep.tile([P, widths[4]], U32, name="codes4", tag="woven1", align_bytes=64))
+        for c in order[2:]:
             quantise(c)
-        ratio = keep.tile([P, V], F32, name="ratio", tag=f"woven{len(pieces) - 1}", align_bytes=64)
+        ratio = keep.tile([P, V], F32, name="ratio", tag="woven3", align_bytes=64)
         nc.vector.tensor_scalar_add(
             ratio[:].rearrange("m (p e) -> m p e", e=4), spread[0][:, :, : P // 2].rearrange("m e p -> m p e"), -1.0
         )
-        for c in range(len(pieces)):
-            project(c, nc.vector.tensor_copy if c == len(pieces) - 1 else nc.scalar.copy)
+        for c in order:
+            project(c, nc.vector.tensor_copy if c == order[-1] else nc.scalar.copy)
 
-        cuts = [0, 192, V]
+        cuts = [0, 128, V]
         parts = list(zip(cuts, cuts[1:]))
         first = [keep.tile([P, hi - lo], F32, name=f"first{lo}") for lo, hi in parts]
         total = [keep.tile([P, hi - lo], F32, name=f"total{lo}") for lo, hi in parts]

@@ -139,12 +139,12 @@ def tile_picked_gatv_relu_e_kernel(
         codes.append(keep.tile([P, widths[4]], U32, name="codes4", tag="woven1", align_bytes=64))
         for c in order[2:]:
             quantise(c)
-        ratio = keep.tile([P, V], F32, name="ratio", tag="woven3", align_bytes=64)
+        ratio = reuse.tile([P, V], F32, name="ratio", offset=0, align_bytes=64)
         nc.vector.tensor_scalar_add(
             ratio[:].rearrange("m (p e) -> m p e", e=4), spread[0][:, :, : P // 2].rearrange("m e p -> m p e"), -1.0
         )
         for c in order:
-            project(c, nc.vector.tensor_copy if c == order[-1] else nc.scalar.copy)
+            project(c, nc.vector.tensor_copy if c == order[-2] else nc.scalar.copy)
 
         cuts = [0, 128, V]
         parts = list(zip(cuts, cuts[1:]))

@@ -22,6 +22,8 @@ PIECE = 128
 PIECES = S // PIECE
 PER_COL = 16
 FLOOR = 2.0**-26
+ROWS = 32
+PER_ROW = V // ROWS
 
 
 def tile_picked_gatv_relu_e_kernel(
@@ -40,8 +42,8 @@ def tile_picked_gatv_relu_e_kernel(
 
         nc.sync.dma_start(planes[2][:], x_rows[:, 2, :])
         nc.sync.dma_start(offs_sb[:], offs)
-        sc = keep.tile([P // 2, 2, 8], F32, name="sc")
-        nc.sync.dma_start(sc[:, :, 0:4], score[:, 0, :].rearrange("d (p e) -> p d e", e=4))
+        sc = keep.tile([ROWS, 2, PER_ROW], F32, name="sc")
+        nc.sync.dma_start(sc[:], score[:, 0, :].rearrange("d (p e) -> p d e", e=PER_ROW))
         nc.sync.dma_start(planes[0][:], x_rows[:, 0, :])
         for t in (1, 3):
             nc.sync.dma_start(planes[t][:], x_rows[:, t, :])
@@ -108,19 +110,22 @@ def tile_picked_gatv_relu_e_kernel(
             copy(y[:, pieces[c]], acc[:])
 
         share = 384
-        a_col = keep.tile([P, 2, 4], F32, name="a_col")
-        nc.gpsimd.memset(a_col[P // 2 :], 0.0)
-        raw = keep.tile([P // 2, 4], F32, name="raw")
-        minus_one = keep.tile([P // 2, 4], F32, name="minus_one")
+        a_col = keep.tile([P, 2, PER_ROW], F32, name="a_col")
+        nc.gpsimd.memset(a_col[:], 0.0)
+        raw = keep.tile([ROWS, PER_ROW], F32, name="raw")
+        minus_one = keep.tile([ROWS, PER_ROW], F32, name="minus_one")
         nc.gpsimd.memset(minus_one[:], -1.0)
-        for e in range(4):
+        for e in range(PER_ROW):
             nc.scalar.activation(raw[:, e : e + 1], sc[:, 0, e : e + 1], ACT.Sigmoid, bias=sc[:, 1, e : e + 1], scale=-1.0)
-        nc.gpsimd.tensor_scalar(a_col[: P // 2, 1, :], raw[:], FLOOR, 1.0, ALU.max, ALU.mult)
-        nc.gpsimd.tensor_tensor(a_col[: P // 2, 0, :], a_col[: P // 2, 1, :], minus_one[:], ALU.pow)
-        spread = [psum.tile([P, 4, P], F32, name=f"spread{d}") for d in range(2)]
-        for d in range(2):
-            for e in range(4):
-                nc.tensor.transpose(spread[d][:, e, :], a_col[:, d, e : e + 1].to_broadcast([P, P]), ident[:])
+        nc.gpsimd.tensor_scalar(a_col[:ROWS, 1, :], raw[:], FLOOR, 1.0, ALU.max, ALU.mult)
+        nc.gpsimd.tensor_tensor(a_col[:ROWS, 0, :], a_col[:ROWS, 1, :], minus_one[:], ALU.pow)
+        spread = [psum.tile([P, V - ROWS + P], F32, name=f"spread{d}") for d in range(2)]
+        for d in (1, 0):
+            for e in range(PER_ROW):
+                nc.tensor.transpose(
+                    spread[d][:, ROWS * e : ROWS * e + P], a_col[:, d, e : e + 1].to_broadcast([P, P]), ident[:]
+                )
+        by_target = [spread[d][:, :V].rearrange("m (e p) -> m p e", p=ROWS) for d in range(2)]
         gather(2, 0, head)
         gather(2, head, S)
         for t in range(2):
@@ -141,7 +146,7 @@ def tile_picked_gatv_relu_e_kernel(
             quantise(c)
         ratio = reuse.tile([P, V], F32, name="ratio", offset=0, align_bytes=64)
         nc.vector.tensor_scalar_add(
-            ratio[:].rearrange("m (p e) -> m p e", e=4), spread[0][:, :, : P // 2].rearrange("m e p -> m p e"), -1.0
+            ratio[:].rearrange("m (p e) -> m p e", e=PER_ROW), by_target[0], -1.0
         )
         for c in order:
             project(c, nc.vector.tensor_copy if c == order[-2] else nc.scalar.copy)
@@ -159,11 +164,10 @@ def tile_picked_gatv_relu_e_kernel(
             nc.vector.tensor_tensor(
                 total[h][:], y[:].indirect(pos_sb[1][:, lo // PER_COL : hi // PER_COL]), first[h][:], ALU.add
             )
-        weight = spread[1][:, :, : P // 2].rearrange("m e p -> m p e")
         for h, (lo, hi) in enumerate(parts):
             nc.vector.scalar_tensor_tensor(
-                result[h][:].rearrange("m (p e) -> m p e", e=4), total[h][:].rearrange("m (p e) -> m p e", e=4), 0.0,
-                weight[:, lo // 4 : hi // 4, :], ALU.max, ALU.mult,
+                result[h][:].rearrange("m (p e) -> m p e", e=PER_ROW), total[h][:].rearrange("m (p e) -> m p e", e=PER_ROW),
+                0.0, by_target[1][:, lo // PER_ROW : hi // PER_ROW, :], ALU.max, ALU.mult,
             )
         nc.sync.dma_start(out[:, cuts[0] : cuts[1]], result[0][:])
         nc.scalar.dma_start(out[:, cuts[1] : cuts[2]], result[1][:])

@@ -32,7 +32,6 @@ def tile_picked_gatv_relu_e_kernel(
     nc = tc.nc
     with ExitStack() as ctx:
         keep = ctx.enter_context(tc.tile_pool(name="keep", bufs=1))
-        reuse = ctx.enter_context(tc.tile_pool(name="reuse", bufs=1))
         psum = ctx.enter_context(tc.psum_pool(name="psum", bufs=1))
 
         offs_sb = keep.tile([P, S // PER_COL], U16, name="offs_sb")
@@ -66,19 +65,14 @@ def tile_picked_gatv_relu_e_kernel(
         bounds = [0, 128, 256, 384, 448, 512]
         pieces = [slice(lo, hi) for lo, hi in zip(bounds, bounds[1:])]
         widths = [hi - lo for lo, hi in zip(bounds, bounds[1:])]
-        head = bounds[1]
-        picked = {
-            0: reuse.tile([P, 2, head, 2], BF16, name="picked_head", offset=0, align_bytes=64),
-            head: keep.tile([P, 2, S - head, 2], BF16, name="picked_rest"),
-        }
+        picked = keep.tile([P, 2, S, 2], BF16, name="picked")
 
         def pairs(lo, hi):
-            start = 0 if lo < head else head
-            return picked[start][:, :, lo - start : hi - start, :]
+            return picked[:, :, lo:hi, :]
 
         rounded = [keep.tile([P, T], BF16, name=f"rounded{t}") for t in range(2)]
-        woven = [keep.tile([P, n, 2], U32, name=f"woven{c}", tag=f"woven{c}", align_bytes=64) for c, n in enumerate(widths[:-1])]
-        codes = [keep.tile([P, n], U32, name=f"codes{c}", tag=f"codes{c}", align_bytes=64) for c, n in enumerate(widths[:-1])]
+        woven = [keep.tile([P, n, 2], U32, name=f"woven{c}", tag=f"woven{c}", align_bytes=64) for c, n in enumerate(widths)]
+        codes = [keep.tile([P, n], U32, name=f"codes{c}", tag=f"codes{c}", align_bytes=64) for c, n in enumerate(widths)]
         scales = [keep.tile([P, n], U8, name=f"scales{c}", align_bytes=64) for c, n in enumerate(widths)]
         y = keep.tile([P, S], F32, name="y")
 
@@ -126,25 +120,18 @@ def tile_picked_gatv_relu_e_kernel(
                     spread[d][:, ROWS * e : ROWS * e + P], a_col[:, d, e : e + 1].to_broadcast([P, P]), ident[:]
                 )
         by_target = [spread[d][:, :V].rearrange("m (e p) -> m p e", p=ROWS) for d in range(2)]
-        gather(2, 0, head)
-        gather(2, head, S)
+        gather(2, 0, S)
         for t in range(2):
-            gather(t, 0, head)
-            gather(t, head, share)
+            gather(t, 0, share)
             gather_rounded(t, share, S)
         for lo in range(0, S, 128):
             gather(3, lo, lo + 128)
-        for c in range(4):
+        order = list(range(len(pieces)))
+        for c in order:
             weave(c, nc.scalar.copy, U32)
-        quantise(0)
-        woven.append(reuse.tile([P, widths[4], 2], U32, name="woven4", offset=0, align_bytes=64))
-        weave(4, nc.vector.tensor_copy, I32)
-        order = [0, 1, 2, 4, 3]
-        quantise(1)
-        codes.append(keep.tile([P, widths[4]], U32, name="codes4", tag="woven1", align_bytes=64))
-        for c in order[2:]:
+        for c in order:
             quantise(c)
-        ratio = reuse.tile([P, V], F32, name="ratio", offset=0, align_bytes=64)
+        ratio = keep.tile([P, V], F32, name="ratio", tag="woven4", align_bytes=64)
         nc.vector.tensor_scalar_add(
             ratio[:].rearrange("m (p e) -> m p e", e=PER_ROW), by_target[0], -1.0
         )

@@ -131,12 +131,14 @@ def tile_picked_gatv_relu_e_kernel(
             weave(c, nc.scalar.copy, U32)
         for c in order:
             quantise(c)
-        ratio = keep.tile([P, V], F32, name="ratio", tag="woven4", align_bytes=64)
+        ratio = keep.tile([P, V], F32, name="ratio", tag="woven3", align_bytes=64)
         nc.vector.tensor_scalar_add(
             ratio[:].rearrange("m (p e) -> m p e", e=PER_ROW), by_target[0], -1.0
         )
         for c in order:
             project(c, nc.vector.tensor_copy if c == order[-2] else nc.scalar.copy)
+        weight = keep.tile([P, V], F32, name="weight", tag="codes4", align_bytes=64)
+        nc.scalar.copy(weight[:].rearrange("m (p e) -> m p e", e=PER_ROW), by_target[1])
 
         cuts = [0, 128, V]
         parts = list(zip(cuts, cuts[1:]))
@@ -153,8 +155,7 @@ def tile_picked_gatv_relu_e_kernel(
             )
         for h, (lo, hi) in enumerate(parts):
             nc.vector.scalar_tensor_tensor(
-                result[h][:].rearrange("m (p e) -> m p e", e=PER_ROW), total[h][:].rearrange("m (p e) -> m p e", e=PER_ROW),
-                0.0, by_target[1][:, lo // PER_ROW : hi // PER_ROW, :], ALU.max, ALU.mult,
+                result[h][:], total[h][:], 0.0, weight[:, lo:hi], ALU.max, ALU.mult,
             )
         nc.sync.dma_start(out[:, cuts[0] : cuts[1]], result[0][:])
         nc.scalar.dma_start(out[:, cuts[1] : cuts[2]], result[1][:])

@@ -39,14 +39,12 @@ def tile_picked_gatv_relu_e_kernel(
         planes = [keep.tile([P, T], F32, name=f"plane{t}") for t in range(PACK)]
         x_rows = xT.rearrange("(p t) n -> p t n", t=PACK)
 
-        nc.sync.dma_start(planes[2][:], x_rows[:, 2, :])
-        nc.sync.dma_start(offs_sb[:], offs)
-        sc = keep.tile([ROWS, 2, PER_ROW], F32, name="sc")
-        nc.sync.dma_start(sc[:], score[:, 0, :].rearrange("d (p e) -> p d e", e=PER_ROW))
         nc.sync.dma_start(planes[0][:], x_rows[:, 0, :])
-        for t in (1, 3):
+        nc.sync.dma_start(offs_sb[:], offs)
+        sc = keep.tile([ROWS, 2, PER_ROW], F32, name="sc", tag="sc")
+        nc.sync.dma_start(sc[:], score[:, 0, :].rearrange("d (p e) -> p d e", e=PER_ROW))
+        for t in range(1, PACK):
             nc.sync.dma_start(planes[t][:], x_rows[:, t, :])
-
 
         w_words = keep.tile([P, M], U32, name="w_words", align_bytes=64)
         w_scales = keep.tile([P, M], U8, name="w_scales", align_bytes=64)
@@ -62,48 +60,48 @@ def tile_picked_gatv_relu_e_kernel(
         ident = keep.tile([P, P], F32, name="ident")
         make_identity(nc, ident[:])
 
-        bounds = [0, 128, 256, 384, 448, 512]
-        pieces = [slice(lo, hi) for lo, hi in zip(bounds, bounds[1:])]
-        widths = [hi - lo for lo, hi in zip(bounds, bounds[1:])]
-        picked = keep.tile([P, 2, S, 2], BF16, name="picked")
-
-        def pairs(lo, hi):
-            return picked[:, :, lo:hi, :]
-
-        rounded = [keep.tile([P, T], BF16, name=f"rounded{t}") for t in range(2)]
-        woven = [keep.tile([P, n, 2], U32, name=f"woven{c}", tag=f"woven{c}", align_bytes=64) for c, n in enumerate(widths)]
-        codes = [keep.tile([P, n], U32, name=f"codes{c}", tag=f"codes{c}", align_bytes=64) for c, n in enumerate(widths)]
-        scales = [keep.tile([P, n], U8, name=f"scales{c}", align_bytes=64) for c, n in enumerate(widths)]
+        half = S // 2
+        pairs = keep.tile([P, 2, half, 2], BF16, name="pairs")
+        early = keep.tile([P, 2, half], BF16, name="early", tag="sc")
+        late = [[keep.tile([P, PIECE], BF16, name=f"late{t}_{c}") for c in range(2)] for t in range(2)]
+        filled = keep.tile([P, half * PACK], BF16, name="filled", align_bytes=64)
+        slots = filled[:].rearrange("p (n t) -> p n t", t=PACK)
+        woven = [keep.tile([P, PIECE, 2], U32, name=f"woven{c}", tag=f"woven{c}", align_bytes=64) for c in range(2)]
+        codes = [keep.tile([P, PIECE], U32, name=f"codes{c}", tag=f"codes{c}", align_bytes=64) for c in range(PIECES)]
+        scales = [keep.tile([P, PIECE], U8, name=f"scales{c}", align_bytes=64) for c in range(PIECES)]
         y = keep.tile([P, S], F32, name="y")
 
-        def entries(lo, hi):
-            return offs_sb[:, lo // PER_COL : hi // PER_COL]
+        def picked(t, lo, hi):
+            return planes[t][:].indirect(offs_sb[:, lo // PER_COL : hi // PER_COL])
 
-        def gather(t, lo, hi):
-            nc.vector.tensor_copy(pairs(lo, hi)[:, t // 2, :, t % 2], planes[t][:].indirect(entries(lo, hi)))
+        def gather_pairs(t, lo, hi):
+            nc.vector.tensor_copy(pairs[:, t // 2, lo:hi, t % 2], picked(t, lo, hi))
 
-        def gather_rounded(t, lo, hi):
-            nc.scalar.copy(rounded[t][:], planes[t][:])
-            nc.scalar.activation(pairs(lo, hi)[:, t // 2, :, t % 2], rounded[t][:].indirect(entries(lo, hi)), ACT.Copy)
+        def gather_late(t, c):
+            nc.scalar.activation(late[t - 2][c][:], picked(t, half + PIECE * c, half + PIECE * (c + 1)), ACT.Copy)
 
-        def weave(c, copy, word):
-            words = pairs(bounds[c], bounds[c + 1]).rearrange("p u n e -> p u (n e)").bitcast(word)
-            copy(woven[c][:].bitcast(word), words.rearrange("p u n -> p n u"))
+        def fill(t, c):
+            nc.vector.tensor_copy(slots[:, PIECE * c : PIECE * (c + 1), t], late[t - 2][c][:])
+
+        def weave(c):
+            words = pairs[:, :, PIECE * c : PIECE * (c + 1), :].rearrange("p u n e -> p u (n e)").bitcast(U32)
+            nc.scalar.copy(woven[c][:], words.rearrange("p u n -> p n u"))
 
         def quantise(c):
-            nc.vector.quantize_mx(
-                out=codes[c][:].bitcast(FP8X4), scales=scales[c][:], in_=woven[c][:].rearrange("p n u -> p (n u)").bitcast(BF16)
-            )
+            if c < 2:
+                rows = woven[c][:].rearrange("p n u -> p (n u)").bitcast(BF16)
+            else:
+                rows = filled[:, PACK * PIECE * (c - 2) : PACK * PIECE * (c - 1)]
+            nc.vector.quantize_mx(out=codes[c][:].bitcast(FP8X4), scales=scales[c][:], in_=rows)
 
         def project(c, copy):
-            acc = psum.tile([M, widths[c]], F32, name=f"acc{c}")
+            acc = psum.tile([M, PIECE], F32, name=f"acc{c}")
             nc.tensor.matmul_mx(
                 out=acc[:], lhsT=w_words[:].bitcast(FP8X4), lhsT_scale=w_scales[:],
                 rhs=codes[c][:].bitcast(FP8X4), rhs_scale=scales[c][:], start=True, stop=True,
             )
-            copy(y[:, pieces[c]], acc[:])
+            copy(y[:, PIECE * c : PIECE * (c + 1)], acc[:])
 
-        share = 384
         a_col = keep.tile([P, 2, PER_ROW], F32, name="a_col")
         nc.gpsimd.memset(a_col[:], 0.0)
         raw = keep.tile([ROWS, PER_ROW], F32, name="raw")
@@ -120,25 +118,32 @@ def tile_picked_gatv_relu_e_kernel(
                     spread[d][:, ROWS * e : ROWS * e + P], a_col[:, d, e : e + 1].to_broadcast([P, P]), ident[:]
                 )
         by_target = [spread[d][:, :V].rearrange("m (e p) -> m p e", p=ROWS) for d in range(2)]
-        gather(2, 0, S)
         for t in range(2):
-            gather(t, 0, share)
-            gather_rounded(t, share, S)
-        for lo in range(0, S, 128):
-            gather(3, lo, lo + 128)
-        order = list(range(len(pieces)))
-        for c in order:
-            weave(c, nc.scalar.copy, U32)
+            gather_pairs(t, 0, half)
+            nc.scalar.activation(early[:, t, :], picked(t, half, S), ACT.Copy)
+        nc.vector.tensor_copy(slots[:, :, 0:2], early[:].rearrange("p t n -> p n t"))
+        gather_pairs(2, 0, half)
+        for c in range(2):
+            gather_late(2, c)
+        for c in range(2):
+            fill(2, c)
+        for c in range(2):
+            gather_pairs(3, PIECE * c, PIECE * (c + 1))
+        for c in range(2):
+            gather_late(3, c)
+        for c in range(2):
+            fill(3, c)
+        for c in range(2):
+            weave(c)
+        order = [2, 0, 3, 1]
         for c in order:
             quantise(c)
-        ratio = keep.tile([P, V], F32, name="ratio", tag="woven3", align_bytes=64)
+        ratio = keep.tile([P, V], F32, name="ratio", tag="woven1", align_bytes=64)
         nc.vector.tensor_scalar_add(
             ratio[:].rearrange("m (p e) -> m p e", e=PER_ROW), by_target[0], -1.0
         )
         for c in order:
-            project(c, nc.vector.tensor_copy if c == order[-2] else nc.scalar.copy)
-        weight = keep.tile([P, V], F32, name="weight", tag="codes4", align_bytes=64)
-        nc.scalar.copy(weight[:].rearrange("m (p e) -> m p e", e=PER_ROW), by_target[1])
+            project(c, nc.scalar.copy)
 
         cuts = [0, 128, V]
         parts = list(zip(cuts, cuts[1:]))
@@ -149,13 +154,16 @@ def tile_picked_gatv_relu_e_kernel(
             nc.vector.tensor_tensor(
                 first[h][:], y[:].indirect(pos_sb[0][:, lo // PER_COL : hi // PER_COL]), ratio[:, lo:hi], ALU.mult
             )
+        second = [keep.tile([P, hi - lo], F32, name=f"second{lo}") for lo, hi in parts]
         for h, (lo, hi) in enumerate(parts):
-            nc.vector.tensor_tensor(
-                total[h][:], y[:].indirect(pos_sb[1][:, lo // PER_COL : hi // PER_COL]), first[h][:], ALU.add
-            )
+            nc.scalar.activation(second[h][:], y[:].indirect(pos_sb[1][:, lo // PER_COL : hi // PER_COL]), ACT.Copy)
+        for h, (lo, hi) in enumerate(parts):
+            nc.vector.tensor_tensor(total[h][:], second[h][:], first[h][:], ALU.add)
         for h, (lo, hi) in enumerate(parts):
             nc.vector.scalar_tensor_tensor(
-                result[h][:], total[h][:], 0.0, weight[:, lo:hi], ALU.max, ALU.mult,
+                result[h][:].rearrange("m (p e) -> m p e", e=PER_ROW),
+                total[h][:].rearrange("m (p e) -> m p e", e=PER_ROW), 0.0,
+                by_target[1][:, lo // PER_ROW : hi // PER_ROW, :], ALU.max, ALU.mult,
             )
         nc.sync.dma_start(out[:, cuts[0] : cuts[1]], result[0][:])
         nc.scalar.dma_start(out[:, cuts[1] : cuts[2]], result[1][:])

@@ -61,14 +61,16 @@ def tile_picked_gatv_relu_e_kernel(
         make_identity(nc, ident[:])
 
         half = S // 2
-        pairs = keep.tile([P, 2, half, 2], BF16, name="pairs")
+        pairs = keep.tile([P, 2, half, 2], BF16, name="pairs", tag="pairs")
         early = keep.tile([P, 2, half], BF16, name="early", tag="sc")
         late = [[keep.tile([P, PIECE], BF16, name=f"late{t}_{c}") for c in range(2)] for t in range(2)]
         filled = keep.tile([P, half * PACK], BF16, name="filled", align_bytes=64)
         slots = filled[:].rearrange("p (n t) -> p n t", t=PACK)
-        woven = [keep.tile([P, PIECE, 2], U32, name=f"woven{c}", tag=f"woven{c}", align_bytes=64) for c in range(2)]
-        codes = [keep.tile([P, PIECE], U32, name=f"codes{c}", tag=f"codes{c}", align_bytes=64) for c in range(PIECES)]
-        scales = [keep.tile([P, PIECE], U8, name=f"scales{c}", align_bytes=64) for c in range(PIECES)]
+        bounds = [0, 128, 192, 256, 384, S]
+        widths = [hi - lo for lo, hi in zip(bounds, bounds[1:])]
+        woven = [keep.tile([P, widths[c], 2], U32, name=f"woven{c}", tag=f"woven{c}", align_bytes=64) for c in range(3)]
+        codes = [keep.tile([P, n], U32, name=f"codes{c}", align_bytes=64) for c, n in enumerate(widths)]
+        scales = [keep.tile([P, n], U8, name=f"scales{c}", align_bytes=64) for c, n in enumerate(widths)]
         y = keep.tile([P, S], F32, name="y")
 
         def picked(t, lo, hi):
@@ -84,38 +86,40 @@ def tile_picked_gatv_relu_e_kernel(
             nc.vector.tensor_copy(slots[:, PIECE * c : PIECE * (c + 1), t], late[t - 2][c][:])
 
         def weave(c):
-            words = pairs[:, :, PIECE * c : PIECE * (c + 1), :].rearrange("p u n e -> p u (n e)").bitcast(U32)
+            words = pairs[:, :, bounds[c] : bounds[c + 1], :].rearrange("p u n e -> p u (n e)").bitcast(U32)
             nc.scalar.copy(woven[c][:], words.rearrange("p u n -> p n u"))
 
         def quantise(c):
-            if c < 2:
+            if c < 3:
                 rows = woven[c][:].rearrange("p n u -> p (n u)").bitcast(BF16)
             else:
-                rows = filled[:, PACK * PIECE * (c - 2) : PACK * PIECE * (c - 1)]
+                rows = filled[:, PACK * (bounds[c] - half) : PACK * (bounds[c + 1] - half)]
             nc.vector.quantize_mx(out=codes[c][:].bitcast(FP8X4), scales=scales[c][:], in_=rows)
 
         def project(c, copy):
-            acc = psum.tile([M, PIECE], F32, name=f"acc{c}")
+            acc = psum.tile([M, widths[c]], F32, name=f"acc{c}")
             nc.tensor.matmul_mx(
                 out=acc[:], lhsT=w_words[:].bitcast(FP8X4), lhsT_scale=w_scales[:],
                 rhs=codes[c][:].bitcast(FP8X4), rhs_scale=scales[c][:], start=True, stop=True,
             )
-            copy(y[:, PIECE * c : PIECE * (c + 1)], acc[:])
+            copy(y[:, bounds[c] : bounds[c + 1]], acc[:])
 
-        a_col = keep.tile([P, 2, PER_ROW], F32, name="a_col")
+        a_col = keep.tile([P, PER_ROW], F32, name="a_col")
+        inverse = keep.tile([P, PER_ROW], F32, name="inverse")
         nc.gpsimd.memset(a_col[:], 0.0)
+        nc.gpsimd.memset(inverse[:], 0.0)
         raw = keep.tile([ROWS, PER_ROW], F32, name="raw")
-        minus_one = keep.tile([ROWS, PER_ROW], F32, name="minus_one")
-        nc.gpsimd.memset(minus_one[:], -1.0)
         for e in range(PER_ROW):
             nc.scalar.activation(raw[:, e : e + 1], sc[:, 0, e : e + 1], ACT.Sigmoid, bias=sc[:, 1, e : e + 1], scale=-1.0)
-        nc.gpsimd.tensor_scalar(a_col[:ROWS, 1, :], raw[:], FLOOR, 1.0, ALU.max, ALU.mult)
-        nc.gpsimd.tensor_tensor(a_col[:ROWS, 0, :], a_col[:ROWS, 1, :], minus_one[:], ALU.pow)
+        nc.gpsimd.tensor_scalar(a_col[:ROWS, :], raw[:], FLOOR, 1.0, ALU.max, ALU.mult)
+        raw_inverse = keep.tile([ROWS, PER_ROW], F32, name="raw_inverse")
+        nc.vector.reciprocal(raw_inverse[:], raw[:])
+        nc.gpsimd.tensor_scalar(inverse[:ROWS, :], raw_inverse[:], 1.0 / FLOOR, -1.0, ALU.min, ALU.add)
         spread = [psum.tile([P, V - ROWS + P], F32, name=f"spread{d}") for d in range(2)]
         for d in (1, 0):
             for e in range(PER_ROW):
                 nc.tensor.transpose(
-                    spread[d][:, ROWS * e : ROWS * e + P], a_col[:, d, e : e + 1].to_broadcast([P, P]), ident[:]
+                    spread[d][:, ROWS * e : ROWS * e + P], (inverse, a_col)[d][:, e : e + 1].to_broadcast([P, P]), ident[:]
                 )
         by_target = [spread[d][:, :V].rearrange("m (e p) -> m p e", p=ROWS) for d in range(2)]
         for t in range(2):
@@ -133,17 +137,17 @@ def tile_picked_gatv_relu_e_kernel(
             gather_late(3, c)
         for c in range(2):
             fill(3, c)
-        for c in range(2):
+        for c in range(3):
             weave(c)
-        order = [2, 0, 3, 1]
+        order = [3, 0, 4, 1, 2]
         for c in order:
             quantise(c)
-        ratio = keep.tile([P, V], F32, name="ratio", tag="woven1", align_bytes=64)
-        nc.vector.tensor_scalar_add(
-            ratio[:].rearrange("m (p e) -> m p e", e=PER_ROW), by_target[0], -1.0
-        )
+        ratio = keep.tile([P, V], F32, name="ratio", tag="pairs")
+        nc.scalar.copy(ratio[:].rearrange("m (p e) -> m p e", e=PER_ROW), by_target[0])
+        weight = keep.tile([P, V], F32, name="weight", tag="woven2", align_bytes=64)
+        nc.vector.tensor_copy(weight[:].rearrange("m (p e) -> m p e", e=PER_ROW), by_target[1])
         for c in order:
-            project(c, nc.scalar.copy)
+            project(c, nc.vector.tensor_copy if c == order[-2] else nc.scalar.copy)
 
         cuts = [0, 128, V]
         parts = list(zip(cuts, cuts[1:]))
@@ -161,9 +165,7 @@ def tile_picked_gatv_relu_e_kernel(
             nc.vector.tensor_tensor(total[h][:], second[h][:], first[h][:], ALU.add)
         for h, (lo, hi) in enumerate(parts):
             nc.vector.scalar_tensor_tensor(
-                result[h][:].rearrange("m (p e) -> m p e", e=PER_ROW),
-                total[h][:].rearrange("m (p e) -> m p e", e=PER_ROW), 0.0,
-                by_target[1][:, lo // PER_ROW : hi // PER_ROW, :], ALU.max, ALU.mult,
+                result[h][:], total[h][:], 0.0, weight[:, lo:hi], ALU.max, ALU.mult,
             )
         nc.sync.dma_start(out[:, cuts[0] : cuts[1]], result[0][:])
         nc.scalar.dma_start(out[:, cuts[1] : cuts[2]], result[1][:])

@@ -63,7 +63,7 @@ def tile_picked_gatv_relu_e_kernel(
         half = S // 2
         pairs = keep.tile([P, 2, half, 2], BF16, name="pairs", tag="pairs")
         early = keep.tile([P, 2, half], BF16, name="early", tag="sc")
-        late = [[keep.tile([P, PIECE], BF16, name=f"late{t}_{c}") for c in range(2)] for t in range(2)]
+        late = [keep.tile([P, 2, PIECE], BF16, name=f"late{c}") for c in range(2)]
         filled = keep.tile([P, half * PACK], BF16, name="filled", align_bytes=64)
         slots = filled[:].rearrange("p (n t) -> p n t", t=PACK)
         bounds = [0, 128, 192, 256, 384, S]
@@ -80,10 +80,10 @@ def tile_picked_gatv_relu_e_kernel(
             nc.vector.tensor_copy(pairs[:, t // 2, lo:hi, t % 2], picked(t, lo, hi))
 
         def gather_late(t, c):
-            nc.scalar.activation(late[t - 2][c][:], picked(t, half + PIECE * c, half + PIECE * (c + 1)), ACT.Copy)
+            nc.scalar.activation(late[c][:, t - 2, :], picked(t, half + PIECE * c, half + PIECE * (c + 1)), ACT.Copy)
 
-        def fill(t, c):
-            nc.vector.tensor_copy(slots[:, PIECE * c : PIECE * (c + 1), t], late[t - 2][c][:])
+        def fill(c):
+            nc.vector.tensor_copy(slots[:, PIECE * c : PIECE * (c + 1), 2:4], late[c][:].rearrange("p t n -> p n t"))
 
         def weave(c):
             words = pairs[:, :, bounds[c] : bounds[c + 1], :].rearrange("p u n e -> p u (n e)").bitcast(U32)
@@ -130,13 +130,11 @@ def tile_picked_gatv_relu_e_kernel(
         for c in range(2):
             gather_late(2, c)
         for c in range(2):
-            fill(2, c)
-        for c in range(2):
             gather_pairs(3, PIECE * c, PIECE * (c + 1))
         for c in range(2):
             gather_late(3, c)
         for c in range(2):
-            fill(3, c)
+            fill(c)
         for c in range(3):
             weave(c)
         order = [3, 0, 4, 1, 2]

@@ -62,7 +62,7 @@ def tile_picked_gatv_relu_e_kernel(
 
         half = S // 2
         pairs = keep.tile([P, 2, half, 2], BF16, name="pairs", tag="pairs")
-        early = keep.tile([P, 2, half], BF16, name="early", tag="sc")
+        early = [keep.tile([P, 2, PIECE], BF16, name=f"early{c}", tag="sc" if c == 1 else "early") for c in range(2)]
         late = [keep.tile([P, 2, PIECE], BF16, name=f"late{c}") for c in range(2)]
         filled = keep.tile([P, half * PACK], BF16, name="filled", align_bytes=64)
         slots = filled[:].rearrange("p (n t) -> p n t", t=PACK)
@@ -122,10 +122,14 @@ def tile_picked_gatv_relu_e_kernel(
                     spread[d][:, ROWS * e : ROWS * e + P], (inverse, a_col)[d][:, e : e + 1].to_broadcast([P, P]), ident[:]
                 )
         by_target = [spread[d][:, :V].rearrange("m (e p) -> m p e", p=ROWS) for d in range(2)]
-        for t in range(2):
-            gather_pairs(t, 0, half)
-            nc.scalar.activation(early[:, t, :], picked(t, half, S), ACT.Copy)
-        nc.vector.tensor_copy(slots[:, :, 0:2], early[:].rearrange("p t n -> p n t"))
+        gather_pairs(0, 0, half)
+        nc.vector.tensor_copy(early[0][:, 0, :], picked(0, half, half + PIECE))
+        nc.scalar.activation(early[1][:, 0, :], picked(0, half + PIECE, S), ACT.Copy)
+        gather_pairs(1, 0, half)
+        for c in range(2):
+            nc.scalar.activation(early[c][:, 1, :], picked(1, half + PIECE * c, half + PIECE * (c + 1)), ACT.Copy)
+        for c in range(2):
+            nc.vector.tensor_copy(slots[:, PIECE * c : PIECE * (c + 1), 0:2], early[c][:].rearrange("p t n -> p n t"))
         gather_pairs(2, 0, half)
         for c in range(2):
             gather_late(2, c)
@@ -147,11 +151,12 @@ def tile_picked_gatv_relu_e_kernel(
         for c in order:
             project(c, nc.vector.tensor_copy if c == order[-2] else nc.scalar.copy)
 
-        cuts = [0, 128, V]
+        cuts = [0, 96, 192, V]
         parts = list(zip(cuts, cuts[1:]))
         first = [keep.tile([P, hi - lo], F32, name=f"first{lo}") for lo, hi in parts]
         total = [keep.tile([P, hi - lo], F32, name=f"total{lo}") for lo, hi in parts]
-        result = [keep.tile([P, hi - lo], F32, name=f"result{lo}") for lo, hi in parts]
+        halves = [keep.tile([P, cuts[1]], F32, name="result0"), keep.tile([P, V - cuts[1]], F32, name="result1")]
+        result = [halves[0][:], halves[1][:, : cuts[2] - cuts[1]], halves[1][:, cuts[2] - cuts[1] :]]
         for h, (lo, hi) in enumerate(parts):
             nc.vector.tensor_tensor(
                 first[h][:], y[:].indirect(pos_sb[0][:, lo // PER_COL : hi // PER_COL]), ratio[:, lo:hi], ALU.mult
@@ -163,7 +168,7 @@ def tile_picked_gatv_relu_e_kernel(
             nc.vector.tensor_tensor(total[h][:], second[h][:], first[h][:], ALU.add)
         for h, (lo, hi) in enumerate(parts):
             nc.vector.scalar_tensor_tensor(
-                result[h][:], total[h][:], 0.0, weight[:, lo:hi], ALU.max, ALU.mult,
+                result[h], total[h][:], 0.0, weight[:, lo:hi], ALU.max, ALU.mult,
             )
-        nc.sync.dma_start(out[:, cuts[0] : cuts[1]], result[0][:])
-        nc.scalar.dma_start(out[:, cuts[1] : cuts[2]], result[1][:])
+        nc.sync.dma_start(out[:, cuts[0] : cuts[1]], halves[0][:])
+        nc.scalar.dma_start(out[:, cuts[1] :], halves[1][:])

@@ -22,7 +22,7 @@ PIECE = 128
 PIECES = S // PIECE
 PER_COL = 16
 FLOOR = 2.0**-26
-ROWS = 32
+ROWS = 64
 PER_ROW = V // ROWS
 
 
@@ -111,10 +111,10 @@ def tile_picked_gatv_relu_e_kernel(
         raw = keep.tile([ROWS, PER_ROW], F32, name="raw")
         for e in range(PER_ROW):
             nc.scalar.activation(raw[:, e : e + 1], sc[:, 0, e : e + 1], ACT.Sigmoid, bias=sc[:, 1, e : e + 1], scale=-1.0)
-        nc.gpsimd.tensor_scalar(a_col[:ROWS, :], raw[:], FLOOR, 1.0, ALU.max, ALU.mult)
         raw_inverse = keep.tile([ROWS, PER_ROW], F32, name="raw_inverse")
         nc.vector.reciprocal(raw_inverse[:], raw[:])
-        nc.gpsimd.tensor_scalar(inverse[:ROWS, :], raw_inverse[:], 1.0 / FLOOR, -1.0, ALU.min, ALU.add)
+        nc.vector.tensor_scalar_max(a_col[:ROWS, :], raw[:], FLOOR)
+        nc.vector.tensor_scalar(inverse[:ROWS, :], raw_inverse[:], 1.0 / FLOOR, -1.0, ALU.min, ALU.add)
         spread = [psum.tile([P, V - ROWS + P], F32, name=f"spread{d}") for d in range(2)]
         for d in (1, 0):
             for e in range(PER_ROW):

@@ -121,7 +121,7 @@ def tile_picked_gatv_relu_e_kernel(
                 nc.tensor.transpose(
                     spread[d][:, ROWS * e : ROWS * e + P], (inverse, a_col)[d][:, e : e + 1].to_broadcast([P, P]), ident[:]
                 )
-        by_target = [spread[d][:, :V].rearrange("m (e p) -> m p e", p=ROWS) for d in range(2)]
+        by_target = [spread[d][:, :V].rearrange("m (e q i) -> m q e i", e=PER_ROW, i=2) for d in range(2)]
         gather_pairs(0, 0, half)
         nc.vector.tensor_copy(early[0][:, 0, :], picked(0, half, half + PIECE))
         nc.scalar.activation(early[1][:, 0, :], picked(0, half + PIECE, S), ACT.Copy)
@@ -145,11 +145,11 @@ def tile_picked_gatv_relu_e_kernel(
         for c in order:
             quantise(c)
         ratio = keep.tile([P, V], F32, name="ratio", tag="pairs")
-        nc.scalar.copy(ratio[:].rearrange("m (p e) -> m p e", e=PER_ROW), by_target[0])
+        nc.scalar.copy(ratio[:].rearrange("m (q i e) -> m q e i", e=PER_ROW, i=2), by_target[0])
         weight = keep.tile([P, V], F32, name="weight", tag="woven2", align_bytes=64)
-        nc.vector.tensor_copy(weight[:].rearrange("m (p e) -> m p e", e=PER_ROW), by_target[1])
+        nc.vector.tensor_copy(weight[:].rearrange("m (q i e) -> m q e i", e=PER_ROW, i=2), by_target[1])
         for c in order:
-            project(c, nc.vector.tensor_copy if c == order[-2] else nc.scalar.copy)
+            project(c, nc.scalar.copy)
 
         cuts = [0, 96, 192, V]
         parts = list(zip(cuts, cuts[1:]))

@@ -170,5 +170,5 @@ def tile_picked_gatv_relu_e_kernel(
             nc.vector.scalar_tensor_tensor(
                 result[h], total[h][:], 0.0, weight[:, lo:hi], ALU.max, ALU.mult,
             )
-        nc.sync.dma_start(out[:, cuts[0] : cuts[1]], halves[0][:])
+        nc.scalar.dma_start(out[:, cuts[0] : cuts[1]], halves[0][:])
         nc.scalar.dma_start(out[:, cuts[1] :], halves[1][:])

@@ -49,13 +49,13 @@ def tile_picked_gatv_relu_e_kernel(
         w_words = keep.tile([P, M], U32, name="w_words", align_bytes=64)
         w_scales = keep.tile([P, M], U8, name="w_scales", align_bytes=64)
         nc.gpsimd.memset(w_scales[:].bitcast(I32), 0)
+        nc.sync.dma_start(pos_sb[1][:], pos2)
         nc.sync.dma_start(w_words[:].bitcast(I32), w1_words[0].rearrange("p n t -> p (n t)").bitcast(I32))
         for q in range(4):
             nc.sync.dma_start(
                 w_scales[32 * q : 32 * q + 4, :].bitcast(I32), w1_scales[0, 4 * q : 4 * q + 4, :].bitcast(I32)
             )
         nc.sync.dma_start(pos_sb[0][:], pos1)
-        nc.sync.dma_start(pos_sb[1][:], pos2)
 
         ident = keep.tile([P, P], F32, name="ident")
         make_identity(nc, ident[:])

@@ -22,8 +22,10 @@ PIECE = 128
 PIECES = S // PIECE
 PER_COL = 16
 FLOOR = 2.0**-26
-ROWS = 64
-PER_ROW = V // ROWS
+QUAD = 32
+QUADS = P // QUAD
+HALVES = V // P
+PAIR_BYTES = S // 2 * PACK * 2
 
 
 def tile_picked_gatv_relu_e_kernel(
@@ -32,6 +34,7 @@ def tile_picked_gatv_relu_e_kernel(
     nc = tc.nc
     with ExitStack() as ctx:
         keep = ctx.enter_context(tc.tile_pool(name="keep", bufs=1))
+        shared = ctx.enter_context(tc.tile_pool(name="shared", bufs=1))
         psum = ctx.enter_context(tc.psum_pool(name="psum", bufs=1))
 
         offs_sb = keep.tile([P, S // PER_COL], U16, name="offs_sb")
@@ -40,9 +43,10 @@ def tile_picked_gatv_relu_e_kernel(
         x_rows = xT.rearrange("(p t) n -> p t n", t=PACK)
 
         nc.sync.dma_start(planes[0][:], x_rows[:, 0, :])
+        rows = shared.tile([P, 2, V // QUADS], F32, name="rows", offset=PAIR_BYTES - 256, align_bytes=64)
+        nc.vector.memset(rows[:], 0.0)
         nc.sync.dma_start(offs_sb[:], offs)
-        sc = keep.tile([ROWS, 2, PER_ROW], F32, name="sc", tag="sc")
-        nc.sync.dma_start(sc[:], score[:, 0, :].rearrange("d (p e) -> p d e", e=PER_ROW))
+        nc.sync.dma_start(rows[QUAD - 1 : P : QUAD], score[:, 0, :].rearrange("d (q j) -> q d j", q=QUADS))
         for t in range(1, PACK):
             nc.sync.dma_start(planes[t][:], x_rows[:, t, :])
 
@@ -60,9 +64,14 @@ def tile_picked_gatv_relu_e_kernel(
         ident = keep.tile([P, P], F32, name="ident")
         make_identity(nc, ident[:])
 
+        turned = keep.tile([P, P], F32, name="turned", tag="early1", align_bytes=64)
+        nc.vector.transpose(turned[:], rows[:].rearrange("p d j -> p (d j)"))
         half = S // 2
-        pairs = keep.tile([P, 2, half, 2], BF16, name="pairs", tag="pairs")
-        early = [keep.tile([P, 2, PIECE], BF16, name=f"early{c}", tag="sc" if c == 1 else "early") for c in range(2)]
+        pairs = shared.tile([P, 2, half, 2], BF16, name="pairs", offset=0)
+        early = [
+            shared.tile([P, 2, PIECE], BF16, name="early0", offset=PAIR_BYTES),
+            keep.tile([P, 2, PIECE], BF16, name="early1", tag="early1", align_bytes=64),
+        ]
         late = [keep.tile([P, 2, PIECE], BF16, name=f"late{c}") for c in range(2)]
         filled = keep.tile([P, half * PACK], BF16, name="filled", align_bytes=64)
         slots = filled[:].rearrange("p (n t) -> p n t", t=PACK)
@@ -104,24 +113,23 @@ def tile_picked_gatv_relu_e_kernel(
             )
             copy(y[:, bounds[c] : bounds[c + 1]], acc[:])
 
-        a_col = keep.tile([P, PER_ROW], F32, name="a_col")
-        inverse = keep.tile([P, PER_ROW], F32, name="inverse")
-        nc.gpsimd.memset(a_col[:], 0.0)
-        nc.gpsimd.memset(inverse[:], 0.0)
-        raw = keep.tile([ROWS, PER_ROW], F32, name="raw")
-        for e in range(PER_ROW):
-            nc.scalar.activation(raw[:, e : e + 1], sc[:, 0, e : e + 1], ACT.Sigmoid, bias=sc[:, 1, e : e + 1], scale=-1.0)
-        raw_inverse = keep.tile([ROWS, PER_ROW], F32, name="raw_inverse")
+        a_col = keep.tile([P, HALVES], F32, name="a_col")
+        inverse = keep.tile([P, HALVES], F32, name="inverse")
+        raw = keep.tile([P, HALVES], F32, name="raw")
+        live = turned[:].rearrange("p (d e j) -> p d e j", d=2, j=QUAD)[:, :, :, QUAD - 1]
+        for e in range(HALVES):
+            nc.scalar.activation(raw[:, e : e + 1], live[:, 0, e : e + 1], ACT.Sigmoid, bias=live[:, 1, e : e + 1], scale=-1.0)
+        raw_inverse = keep.tile([P, HALVES], F32, name="raw_inverse")
         nc.vector.reciprocal(raw_inverse[:], raw[:])
-        nc.vector.tensor_scalar_max(a_col[:ROWS, :], raw[:], FLOOR)
-        nc.vector.tensor_scalar(inverse[:ROWS, :], raw_inverse[:], 1.0 / FLOOR, -1.0, ALU.min, ALU.add)
-        spread = [psum.tile([P, V - ROWS + P], F32, name=f"spread{d}") for d in range(2)]
+        nc.vector.tensor_scalar_max(a_col[:], raw[:], FLOOR)
+        nc.vector.tensor_scalar(inverse[:], raw_inverse[:], 1.0 / FLOOR, -1.0, ALU.min, ALU.add)
+        spread = [psum.tile([P, V], F32, name=f"spread{d}") for d in range(2)]
         for d in (1, 0):
-            for e in range(PER_ROW):
+            for e in range(HALVES):
                 nc.tensor.transpose(
-                    spread[d][:, ROWS * e : ROWS * e + P], (inverse, a_col)[d][:, e : e + 1].to_broadcast([P, P]), ident[:]
+                    spread[d][:, P * e : P * (e + 1)], (inverse, a_col)[d][:, e : e + 1].to_broadcast([P, P]), ident[:]
                 )
-        by_target = [spread[d][:, :V].rearrange("m (e q i) -> m q e i", e=PER_ROW, i=2) for d in range(2)]
+        by_target = [spread[d][:].rearrange("m (e q j) -> m q e j", e=HALVES, j=QUAD) for d in range(2)]
         gather_pairs(0, 0, half)
         nc.vector.tensor_copy(early[0][:, 0, :], picked(0, half, half + PIECE))
         nc.scalar.activation(early[1][:, 0, :], picked(0, half + PIECE, S), ACT.Copy)
@@ -144,10 +152,10 @@ def tile_picked_gatv_relu_e_kernel(
         order = [3, 0, 4, 1, 2]
         for c in order:
             quantise(c)
-        ratio = keep.tile([P, V], F32, name="ratio", tag="pairs")
-        nc.scalar.copy(ratio[:].rearrange("m (q i e) -> m q e i", e=PER_ROW, i=2), by_target[0])
+        ratio = shared.tile([P, V], F32, name="ratio", offset=0)
+        nc.scalar.copy(ratio[:].rearrange("m (q e j) -> m q e j", e=HALVES, j=QUAD), by_target[0])
         weight = keep.tile([P, V], F32, name="weight", tag="woven2", align_bytes=64)
-        nc.vector.tensor_copy(weight[:].rearrange("m (q i e) -> m q e i", e=PER_ROW, i=2), by_target[1])
+        nc.vector.tensor_copy(weight[:].rearrange("m (q e j) -> m q e j", e=HALVES, j=QUAD), by_target[1])
         for c in order:
             project(c, nc.scalar.copy)
 

@@ -157,7 +157,7 @@ def tile_picked_gatv_relu_e_kernel(
         weight = keep.tile([P, V], F32, name="weight", tag="woven2", align_bytes=64)
         nc.vector.tensor_copy(weight[:].rearrange("m (q e j) -> m q e j", e=HALVES, j=QUAD), by_target[1])
         for c in order:
-            project(c, nc.scalar.copy)
+            project(c, nc.vector.tensor_copy if c == order[2] else nc.scalar.copy)
 
         cuts = [0, 96, 192, V]
         parts = list(zip(cuts, cuts[1:]))

@@ -91,8 +91,10 @@ def tile_picked_gatv_relu_e_kernel(
         def gather_late(t, c):
             nc.scalar.activation(late[c][:, t - 2, :], picked(t, half + PIECE * c, half + PIECE * (c + 1)), ACT.Copy)
 
-        def fill(c):
-            nc.vector.tensor_copy(slots[:, PIECE * c : PIECE * (c + 1), 2:4], late[c][:].rearrange("p t n -> p n t"))
+        def fill(c, lo, hi):
+            nc.vector.tensor_copy(
+                slots[:, PIECE * c : PIECE * (c + 1), lo:hi], late[c][:, lo - 2 : hi - 2, :].rearrange("p t n -> p n t")
+            )
 
         def weave(c):
             words = pairs[:, :, bounds[c] : bounds[c + 1], :].rearrange("p u n e -> p u (n e)").bitcast(U32)
@@ -119,10 +121,8 @@ def tile_picked_gatv_relu_e_kernel(
         live = turned[:].rearrange("p (d e j) -> p d e j", d=2, j=QUAD)[:, :, :, QUAD - 1]
         for e in range(HALVES):
             nc.scalar.activation(raw[:, e : e + 1], live[:, 0, e : e + 1], ACT.Sigmoid, bias=live[:, 1, e : e + 1], scale=-1.0)
-        raw_inverse = keep.tile([P, HALVES], F32, name="raw_inverse")
-        nc.vector.reciprocal(raw_inverse[:], raw[:])
         nc.vector.tensor_scalar_max(a_col[:], raw[:], FLOOR)
-        nc.vector.tensor_scalar(inverse[:], raw_inverse[:], 1.0 / FLOOR, -1.0, ALU.min, ALU.add)
+        nc.vector.reciprocal(inverse[:], a_col[:])
         spread = [psum.tile([P, V], F32, name=f"spread{d}") for d in range(2)]
         for d in (1, 0):
             for e in range(HALVES):
@@ -139,21 +139,24 @@ def tile_picked_gatv_relu_e_kernel(
         for c in range(2):
             nc.vector.tensor_copy(slots[:, PIECE * c : PIECE * (c + 1), 0:2], early[c][:].rearrange("p t n -> p n t"))
         gather_pairs(2, 0, half)
-        for c in range(2):
+        for c in (1, 0):
             gather_late(2, c)
+        fill(1, 2, 3)
         for c in range(2):
             gather_pairs(3, PIECE * c, PIECE * (c + 1))
         for c in range(2):
             gather_late(3, c)
-        for c in range(2):
-            fill(c)
+        fill(0, 2, 4)
+        fill(1, 3, 4)
         for c in range(3):
             weave(c)
         order = [3, 0, 4, 1, 2]
         for c in order:
             quantise(c)
         ratio = shared.tile([P, V], F32, name="ratio", offset=0)
-        nc.scalar.copy(ratio[:].rearrange("m (q e j) -> m q e j", e=HALVES, j=QUAD), by_target[0])
+        nc.scalar.activation(
+            ratio[:].rearrange("m (q e j) -> m q e j", e=HALVES, j=QUAD), by_target[0], ACT.Copy, bias=-1.0
+        )
         weight = keep.tile([P, V], F32, name="weight", tag="woven2", align_bytes=64)
         nc.vector.tensor_copy(weight[:].rearrange("m (q e j) -> m q e j", e=HALVES, j=QUAD), by_target[1])
         for c in order:

from contextlib import ExitStack

import concourse.mybir as mybir
from concourse.masks import make_identity

K, T, S, V, M = 512, 1024, 512, 256, 128
FLOPS = 2 * K * S * M + 4 * M * V

F32 = mybir.dt.float32
BF16 = mybir.dt.bfloat16
I32 = mybir.dt.int32
U32 = mybir.dt.uint32
U16 = mybir.dt.uint16
U8 = mybir.dt.uint8
FP8X4 = mybir.dt.float8_e4m3fn_x4
ACT = mybir.ActivationFunctionType
ALU = mybir.AluOpType

P = 128
PACK = 4
PIECE = 128
PIECES = S // PIECE
PER_COL = 16
FLOOR = 2.0**-26
QUAD = 32
QUADS = P // QUAD
HALVES = V // P
PAIR_BYTES = S // 2 * PACK * 2


def tile_picked_gatv_relu_e_kernel(
    tc, xT, w1_words, w1_scales, score, offs, pos1, pos2, out
):
    nc = tc.nc
    with ExitStack() as ctx:
        keep = ctx.enter_context(tc.tile_pool(name="keep", bufs=1))
        shared = ctx.enter_context(tc.tile_pool(name="shared", bufs=1))
        psum = ctx.enter_context(tc.psum_pool(name="psum", bufs=1))

        offs_sb = keep.tile([P, S // PER_COL], U16, name="offs_sb")
        pos_sb = [keep.tile([P, V // PER_COL], U16, name=f"pos_sb{d}") for d in range(2)]
        planes = [keep.tile([P, T], F32, name=f"plane{t}") for t in range(PACK)]
        x_rows = xT.rearrange("(p t) n -> p t n", t=PACK)

        nc.sync.dma_start(planes[0][:], x_rows[:, 0, :])
        rows = shared.tile([P, 2, V // QUADS], F32, name="rows", offset=PAIR_BYTES - 256, align_bytes=64)
        nc.vector.memset(rows[:], 0.0)
        nc.sync.dma_start(offs_sb[:], offs)
        nc.sync.dma_start(rows[QUAD - 1 : P : QUAD], score[:, 0, :].rearrange("d (q j) -> q d j", q=QUADS))
        for t in range(1, PACK):
            nc.sync.dma_start(planes[t][:], x_rows[:, t, :])

        w_words = keep.tile([P, M], U32, name="w_words", align_bytes=64)
        w_scales = keep.tile([P, M], U8, name="w_scales", align_bytes=64)
        nc.gpsimd.memset(w_scales[:].bitcast(I32), 0)
        nc.sync.dma_start(pos_sb[1][:], pos2)
        nc.sync.dma_start(w_words[:].bitcast(I32), w1_words[0].rearrange("p n t -> p (n t)").bitcast(I32))
        for q in range(4):
            nc.sync.dma_start(
                w_scales[32 * q : 32 * q + 4, :].bitcast(I32), w1_scales[0, 4 * q : 4 * q + 4, :].bitcast(I32)
            )
        nc.sync.dma_start(pos_sb[0][:], pos1)

        ident = keep.tile([P, P], F32, name="ident")
        make_identity(nc, ident[:])

        turned = keep.tile([P, P], F32, name="turned", tag="early1", align_bytes=64)
        nc.vector.transpose(turned[:], rows[:].rearrange("p d j -> p (d j)"))
        half = S // 2
        pairs = shared.tile([P, 2, half, 2], BF16, name="pairs", offset=0)
        early = [
            shared.tile([P, 2, PIECE], BF16, name="early0", offset=PAIR_BYTES),
            keep.tile([P, 2, PIECE], BF16, name="early1", tag="early1", align_bytes=64),
        ]
        late = [keep.tile([P, 2, PIECE], BF16, name=f"late{c}") for c in range(2)]
        filled = keep.tile([P, half * PACK], BF16, name="filled", align_bytes=64)
        slots = filled[:].rearrange("p (n t) -> p n t", t=PACK)
        bounds = [0, 128, 192, 256, 384, S]
        widths = [hi - lo for lo, hi in zip(bounds, bounds[1:])]
        woven = [keep.tile([P, widths[c], 2], U32, name=f"woven{c}", tag=f"woven{c}", align_bytes=64) for c in range(3)]
        codes = [keep.tile([P, n], U32, name=f"codes{c}", align_bytes=64) for c, n in enumerate(widths)]
        scales = [keep.tile([P, n], U8, name=f"scales{c}", align_bytes=64) for c, n in enumerate(widths)]
        y = keep.tile([P, S], F32, name="y")

        def picked(t, lo, hi):
            return planes[t][:].indirect(offs_sb[:, lo // PER_COL : hi // PER_COL])

        def gather_pairs(t, lo, hi):
            nc.vector.tensor_copy(pairs[:, t // 2, lo:hi, t % 2], picked(t, lo, hi))

        def gather_late(t, c):
            nc.scalar.activation(late[c][:, t - 2, :], picked(t, half + PIECE * c, half + PIECE * (c + 1)), ACT.Copy)

        def fill(c, lo, hi):
            nc.vector.tensor_copy(
                slots[:, PIECE * c : PIECE * (c + 1), lo:hi], late[c][:, lo - 2 : hi - 2, :].rearrange("p t n -> p n t")
            )

        def weave(c):
            words = pairs[:, :, bounds[c] : bounds[c + 1], :].rearrange("p u n e -> p u (n e)").bitcast(U32)
            nc.scalar.copy(woven[c][:], words.rearrange("p u n -> p n u"))

        def quantise(c):
            if c < 3:
                rows = woven[c][:].rearrange("p n u -> p (n u)").bitcast(BF16)
            else:
                rows = filled[:, PACK * (bounds[c] - half) : PACK * (bounds[c + 1] - half)]
            nc.vector.quantize_mx(out=codes[c][:].bitcast(FP8X4), scales=scales[c][:], in_=rows)

        def project(c, copy):
            acc = psum.tile([M, widths[c]], F32, name=f"acc{c}")
            nc.tensor.matmul_mx(
                out=acc[:], lhsT=w_words[:].bitcast(FP8X4), lhsT_scale=w_scales[:],
                rhs=codes[c][:].bitcast(FP8X4), rhs_scale=scales[c][:], start=True, stop=True,
            )
            copy(y[:, bounds[c] : bounds[c + 1]], acc[:])

        a_col = keep.tile([P, HALVES], F32, name="a_col")
        inverse = keep.tile([P, HALVES], F32, name="inverse")
        raw = keep.tile([P, HALVES], F32, name="raw")
        live = turned[:].rearrange("p (d e j) -> p d e j", d=2, j=QUAD)[:, :, :, QUAD - 1]
        for e in range(HALVES):
            nc.scalar.activation(raw[:, e : e + 1], live[:, 0, e : e + 1], ACT.Sigmoid, bias=live[:, 1, e : e + 1], scale=-1.0)
        nc.vector.tensor_scalar_max(a_col[:], raw[:], FLOOR)
        nc.vector.reciprocal(inverse[:], a_col[:])
        spread = [psum.tile([P, V], F32, name=f"spread{d}") for d in range(2)]
        for d in (1, 0):
            for e in range(HALVES):
                nc.tensor.transpose(
                    spread[d][:, P * e : P * (e + 1)], (inverse, a_col)[d][:, e : e + 1].to_broadcast([P, P]), ident[:]
                )
        by_target = [spread[d][:].rearrange("m (e q j) -> m q e j", e=HALVES, j=QUAD) for d in range(2)]
        gather_pairs(0, 0, half)
        nc.vector.tensor_copy(early[0][:, 0, :], picked(0, half, half + PIECE))
        nc.scalar.activation(early[1][:, 0, :], picked(0, half + PIECE, S), ACT.Copy)
        gather_pairs(1, 0, half)
        for c in range(2):
            nc.scalar.activation(early[c][:, 1, :], picked(1, half + PIECE * c, half + PIECE * (c + 1)), ACT.Copy)
        for c in range(2):
            nc.vector.tensor_copy(slots[:, PIECE * c : PIECE * (c + 1), 0:2], early[c][:].rearrange("p t n -> p n t"))
        gather_pairs(2, 0, half)
        for c in (1, 0):
            gather_late(2, c)
        fill(1, 2, 3)
        for c in range(2):
            gather_pairs(3, PIECE * c, PIECE * (c + 1))
        for c in range(2):
            gather_late(3, c)
        fill(0, 2, 4)
        fill(1, 3, 4)
        for c in range(3):
            weave(c)
        order = [3, 0, 4, 1, 2]
        for c in order:
            quantise(c)
        ratio = shared.tile([P, V], F32, name="ratio", offset=0)
        nc.scalar.activation(
            ratio[:].rearrange("m (q e j) -> m q e j", e=HALVES, j=QUAD), by_target[0], ACT.Copy, bias=-1.0
        )
        weight = keep.tile([P, V], F32, name="weight", tag="woven2", align_bytes=64)
        nc.vector.tensor_copy(weight[:].rearrange("m (q e j) -> m q e j", e=HALVES, j=QUAD), by_target[1])
        for c in order:
            project(c, nc.vector.tensor_copy if c == order[2] else nc.scalar.copy)

        cuts = [0, 96, 192, V]
        parts = list(zip(cuts, cuts[1:]))
        first = [keep.tile([P, hi - lo], F32, name=f"first{lo}") for lo, hi in parts]
        total = [keep.tile([P, hi - lo], F32, name=f"total{lo}") for lo, hi in parts]
        halves = [keep.tile([P, cuts[1]], F32, name="result0"), keep.tile([P, V - cuts[1]], F32, name="result1")]
        result = [halves[0][:], halves[1][:, : cuts[2] - cuts[1]], halves[1][:, cuts[2] - cuts[1] :]]
        for h, (lo, hi) in enumerate(parts):
            nc.vector.tensor_tensor(
                first[h][:], y[:].indirect(pos_sb[0][:, lo // PER_COL : hi // PER_COL]), ratio[:, lo:hi], ALU.mult
            )
        second = [keep.tile([P, hi - lo], F32, name=f"second{lo}") for lo, hi in parts]
        for h, (lo, hi) in enumerate(parts):
            nc.scalar.activation(second[h][:], y[:].indirect(pos_sb[1][:, lo // PER_COL : hi // PER_COL]), ACT.Copy)
        for h, (lo, hi) in enumerate(parts):
            nc.vector.tensor_tensor(total[h][:], second[h][:], first[h][:], ALU.add)
        for h, (lo, hi) in enumerate(parts):
            nc.vector.scalar_tensor_tensor(
                result[h], total[h][:], 0.0, weight[:, lo:hi], ALU.max, ALU.mult,
            )
        nc.scalar.dma_start(out[:, cuts[0] : cuts[1]], halves[0][:])
        nc.scalar.dma_start(out[:, cuts[1] :], halves[1][:])
